import numpy as np
import ml_dtypes


def mxq(x, axis, fmt="e4m3"):
    dtype, down = {"e4m3": (ml_dtypes.float8_e4m3fn, 7), "e5m2": (ml_dtypes.float8_e5m2, 14)}[fmt]
    v = np.moveaxis(np.asarray(x, np.float32).astype(ml_dtypes.bfloat16).astype(np.float64), axis, -1)
    blocks = v.reshape(v.shape[:-1] + (-1, 32))
    amax = np.abs(blocks).max(-1, keepdims=True)
    byte = np.maximum(np.where(amax > 0, np.frexp(amax)[1] - 1 + 127, 0) - down, 1)
    scale = np.exp2(byte - 127.0)
    codes = (blocks / scale).astype(np.float32).astype(dtype).astype(np.float64)
    return np.moveaxis((codes * scale).reshape(v.shape), -1, axis)


WIDE = False


def mx_kscale(k):
    if not WIDE:
        return np.ones(k)
    levels = np.array([10, -10, 5, -5, 0])
    if k % 512:
        return np.exp2(np.random.permutation(np.resize(levels, k // 32))).repeat(32)
    a = np.empty((k // 512, 16))
    for p in range(k // 512):
        a[p, :8] = np.random.permutation(np.resize(levels, 8))
        for g in range(8):
            far = levels[np.abs(levels - a[p, g]) >= 10]
            a[p, g + 8] = far[np.random.randint(len(far))]
    return np.exp2(a.ravel()).repeat(32)


def f64(x):
    return np.asarray(x).astype(np.float64)


def striped(idx):
    return np.tile(idx.reshape(-1, 16).T, (8, 1)).astype(np.uint16)


def unstriped(offs):
    return offs[:16].T.reshape(-1).astype(np.int64)


E2M1 = np.array([0.0, 0.5, 1.0, 1.5, 2.0, 3.0, 4.0, 6.0, -0.0, -0.5, -1.0, -1.5, -2.0, -3.0, -4.0, -6.0])


def pack_weight(w, fmt):
    k, n = w.shape
    w = f64(np.asarray(w, np.float32).astype(ml_dtypes.bfloat16)).reshape(k // 32, 32, n)
    amax = np.abs(w).max(1)
    if fmt == "e4m3":
        byte = np.frexp(amax)[1] - 1 + 127 - 7
    else:
        mant, ex = np.frexp(amax / 6.0)
        byte = np.where(mant > 0.5, ex, ex - 1) + 127
    byte = np.clip(np.where(amax > 0, byte, 1), 1, 254)
    scaled = (w * np.exp2(127.0 - byte)[:, None, :]).reshape(k, n).astype(np.float32)
    by_word = np.ascontiguousarray(scaled.reshape(k // 512, 128, 4, n).transpose(0, 1, 3, 2))
    if fmt == "e4m3":
        words = by_word.astype(ml_dtypes.float8_e4m3fn).view(np.uint8)
    else:
        c = by_word.astype(ml_dtypes.float4_e2m1fn).view(np.uint8) & 0xF
        words = (c[..., 0::2] | (c[..., 1::2] << 4)).reshape(k // 512, 128, 2 * n)
    return np.ascontiguousarray(words), np.ascontiguousarray(byte.astype(np.uint8).reshape(k // 512, 16, n))


def unpack_weight(words, scales, fmt):
    g, _, n = scales.shape
    words = np.ascontiguousarray(words).reshape(g, 128, n, -1)
    if fmt == "e4m3":
        vals = words.view(ml_dtypes.float8_e4m3fn).astype(np.float64)
    else:
        nib = np.empty((g, 128, n, 4), np.uint8)
        nib[..., 0::2] = words & 0xF
        nib[..., 1::2] = words >> 4
        vals = E2M1[nib]
    vals = vals * np.repeat(np.exp2(scales.astype(np.float64) - 127.0), 8, axis=1)[..., None]
    return vals.transpose(0, 1, 3, 2).reshape(g * 512, n)


def silu(v):
    return v / (1.0 + np.exp(-np.maximum(v, -700.0)))


K, T, E, C, F, D, H = 1024, 512, 8, 128, 4, 128, 512
N = 128


def by_expert(wq, xq, E, C):
    return np.concatenate([wq[e].T @ xq[:, e * C:(e + 1) * C] for e in range(E)], axis=1)


def setup_inputs():
    n = np.random.standard_normal
    s = mx_kscale(K)
    u = mx_kscale(H)
    first = np.random.permutation(np.repeat(np.arange(E), T // E))
    second = (first + 1 + np.random.permutation(np.repeat(np.arange(E - 1), -(-T // (E - 1)))[:T])) % E
    while np.bincount(second, minlength=E).max() != T // E:
        load = np.bincount(second, minlength=E); hi, lo = int(load.argmax()), int(load.argmin())
        t = np.flatnonzero((second == hi) & (first != lo))[0]; second[t] = lo
    slot_token = np.empty(E * C, np.int64); pos = np.empty((2, T), np.int64); fill = np.zeros(E, np.int64)
    place = np.stack([np.random.permutation(C) for _ in range(E)])
    for r, deal in enumerate((first, second)):
        for t in np.random.permutation(T):
            e = deal[t]; j = e * C + place[e, fill[e]]; fill[e] += 1; slot_token[j] = t; pos[r, t] = j
    g = np.random.uniform(0.2, 0.8, T)
    slots2 = np.random.permutation(T)[:F * D]
    x = pack_weight(n((K, T)) * s[:, None], "e4m3")
    w = [pack_weight(m, "e4m3") for m in n((E, K, N)) / np.sqrt(K) / s[None, :, None]]
    wa = [pack_weight(m, "e2m1") for m in n((F, K, H)) / np.sqrt(K) / s[None, :, None] * u]
    wb = [pack_weight(m, "e2m1") for m in n((F, H, N)) / np.sqrt(H) / u[None, :, None]]
    return {
        "x_words": x[0],
        "x_scales": x[1],
        "w_words": np.stack([m[0] for m in w]),
        "w_scales": np.stack([m[1] for m in w]),
        "wa_words": np.stack([m[0] for m in wa]),
        "wa_scales": np.stack([m[1] for m in wa]),
        "wb_words": np.stack([m[0] for m in wb]),
        "wb_scales": np.stack([m[1] for m in wb]),
        "gate": np.stack([np.tile(g, (128, 1)), np.tile(1.0 - g, (128, 1))]).astype(np.float32),
        "gate2": (np.tile(np.random.uniform(0.2, 1.0, F * D), (128, 1))).astype(np.float32),
        "offs": striped(slot_token),
        "pos1": striped(pos[0]),
        "pos2": striped(pos[1]),
        "offs2": striped(slots2),
    }


def reference(x_words, x_scales, w_words, w_scales, wa_words, wa_scales, wb_words, wb_scales, gate, gate2, offs, pos1, pos2, offs2):
    w = np.stack([unpack_weight(w_words[e], w_scales[e], "e4m3") for e in range(E)])
    wa = np.stack([unpack_weight(wa_words[e], wa_scales[e], "e2m1") for e in range(F)])
    wb = np.stack([unpack_weight(wb_words[e], wb_scales[e], "e2m1") for e in range(F)])
    idx, idx2 = unstriped(offs), unstriped(offs2)
    x = unpack_weight(x_words, x_scales, "e4m3")
    y = by_expert(w, x[:, idx], E, C)
    h = silu(by_expert(wa, x[:, idx2], F, D))
    z = by_expert(wb, mxq(h, 0, "e4m3"), F, D)
    out = sum(f64(gate[r, :1]) * y[:, unstriped(p)] for r, p in enumerate((pos1, pos2)))
    out[:, idx2] += f64(gate2[:1]) * z
    return out

@@ -1,0 +1,217 @@
+from contextlib import ExitStack
+
+import concourse.mybir as mybir
+from concourse.masks import make_identity
+
+K, T, E, C, F, D, H, N = 1024, 512, 8, 128, 4, 128, 512, 128
+FLOPS = 2 * K * N * E * C + 2 * K * H * F * D + 2 * H * N * F * D
+
+F32 = mybir.dt.float32
+BF16 = mybir.dt.bfloat16
+I32 = mybir.dt.int32
+U32 = mybir.dt.uint32
+U16 = mybir.dt.uint16
+U8 = mybir.dt.uint8
+FP8X4 = mybir.dt.float8_e4m3fn_x4
+FP4X4 = mybir.dt.float4_e2m1fn_x4
+ACT = mybir.ActivationFunctionType
+ALU = mybir.AluOpType
+
+P = 128
+PASSES = 2
+WINDOW = 704
+HALF = 512
+
+
+def tile_moe_mlr_silu_kernel(
+    tc, x_words, x_scales, w_words, w_scales, wa_words, wa_scales, wb_words, wb_scales,
+    gate, gate2, offs, pos1, pos2, offs2, out
+):
+    nc = tc.nc
+    with ExitStack() as ctx:
+        keep = ctx.enter_context(tc.tile_pool(name="keep", bufs=1))
+        psum = ctx.enter_context(tc.psum_pool(name="psum", bufs=1))
+
+        reuse = ctx.enter_context(tc.tile_pool(name="reuse", bufs=1))
+
+        def sb(name, shape, dtype, tag=None, at=None):
+            if at is not None:
+                return reuse.tile(shape, dtype, name=name, offset=at, align_bytes=64)
+            return keep.tile(shape, dtype, name=name, tag=tag or name, align_bytes=64)
+
+        offs_sb = keep.tile([P, E * C // 16], U16, name="offs_sb")
+        offs2_sb = keep.tile([P, T // 16], U16, name="offs2_sb")
+        pos_sb = [keep.tile([P, T // 16], U16, name=f"pos{r}_sb") for r in (1, 2)]
+
+        x_sb = [sb(f"x_sb{s}", [P, WINDOW], I32) for s in range(PASSES)]
+        xs_apart = sb("xs_apart", [P, T + WINDOW], U8)
+        xs_packed = sb("xs_packed", [P, WINDOW], U8)
+        wa_sb = [sb(f"wa_sb{h}", [P, 4, 2 * H], U8) for h in range(2)]
+        wa_sc = sb("wa_sc", [P, F * PASSES, H], U8)
+        w_sb = [sb(f"w_sb{h}", [P, 8, N], I32) for h in range(2)]
+        w_sc = sb("w_sc", [P, E * PASSES, N], U8)
+        wb_sb = sb("wb_sb", [P, F, 2 * N], U8)
+        wb_sc = sb("wb_sc", [P, F, N], U8)
+        gate_rows = sb("gate_rows", [P, P], F32)
+        gate2_sb = sb("gate2_sb", [P, T], F32)
+        ident = sb("ident", [P, P], F32)
+
+        nc.vector.memset(xs_apart[:].bitcast(I32), 0)
+        for s in range(PASSES):
+            nc.vector.memset(x_sb[s][:, T:WINDOW], 0)
+        nc.gpsimd.memset(wa_sc[:].rearrange("p a i -> p (a i)").bitcast(I32), 0)
+        nc.vector.memset(xs_packed[:].bitcast(I32), 0)
+        nc.gpsimd.memset(w_sc[:].rearrange("p a i -> p (a i)").bitcast(I32), 0)
+        nc.gpsimd.memset(wb_sc[:].rearrange("p a i -> p (a i)").bitcast(I32), 0)
+        nc.gpsimd.memset(gate_rows[:], 0.0)
+        make_identity(nc, ident[:])
+
+        def load_scale_rows(plane, rows):
+            for j in range(4):
+                nc.sync.dma_start(out=plane[j:P:32].bitcast(I32), in_=rows[j].bitcast(I32))
+
+        x_view = x_words.rearrange("s p t d -> s p (t d)").bitcast(I32)
+        wa_view = wa_words.rearrange("f s p b -> p (f s) b").bitcast(I32)
+        w_view = w_words.rearrange("e s p n d -> p (e s) (n d)").bitcast(I32)
+
+        nc.sync.dma_start(offs2_sb[:], offs2)
+        nc.sync.dma_start(out=x_sb[0][:, 0:T], in_=x_view[0])
+        load_scale_rows(xs_apart[:, 0 : PASSES * T].rearrange("p (s t) -> p s t", s=PASSES),
+                        x_scales.rearrange("s (q j) t -> j q s t", j=4))
+        nc.sync.dma_start(out=x_sb[1][:, 0:T], in_=x_view[1])
+        nc.sync.dma_start(out=wa_sb[0][:].bitcast(I32), in_=wa_view[:, 0:4, :])
+        load_scale_rows(wa_sc[:], wa_scales.rearrange("f s (q j) i -> j q (f s) i", j=4))
+        nc.sync.dma_start(offs_sb[:], offs)
+        nc.sync.dma_start(out=wa_sb[1][:].bitcast(I32), in_=wa_view[:, 4:8, :])
+        for q in range(4):
+            nc.sync.dma_start(out=xs_packed[32 * q : 32 * q + 8, 0:T].bitcast(I32),
+                              in_=x_scales[:, 4 * q : 4 * q + 4, :].bitcast(I32))
+        nc.sync.dma_start(out=wb_sb[:].bitcast(I32), in_=wb_words.rearrange("f s p b -> p (f s) b").bitcast(I32))
+        load_scale_rows(wb_sc[:], wb_scales.rearrange("f s (q j) n -> j q (f s) n", j=4))
+        nc.sync.dma_start(out=gate2_sb[:], in_=gate2)
+        nc.sync.dma_start(out=w_sb[0][:], in_=w_view[:, 0:8, :])
+        load_scale_rows(w_sc[:], w_scales.rearrange("e s (q j) n -> j q (e s) n", j=4))
+        nc.sync.dma_start(out=w_sb[1][:], in_=w_view[:, 8:16, :])
+        nc.sync.dma_start(out=gate_rows[0:8, :], in_=gate[:, 0, :].rearrange("r (c t) -> r c t", t=P))
+        nc.sync.dma_start(pos_sb[0][:], pos1)
+        nc.sync.dma_start(pos_sb[1][:], pos2)
+
+        a_words = [sb(f"a_words{s}", [P, T], U32) for s in range(PASSES)]
+        a_scales = [sb(f"a_scales{s}", [P, T], U8) for s in range(PASSES)]
+        for s in range(PASSES):
+            nc.vector.tensor_copy(a_scales[s][:], xs_apart[:, s * T : s * T + WINDOW].indirect(offs2_sb[:]))
+            nc.vector.tensor_copy(a_words[s][:], x_sb[s][:].bitcast(U32).indirect(offs2_sb[:]))
+
+        pre = [psum.tile([P, H], F32, name=f"pre{f}", tag="wide", bufs=4) for f in range(F)]
+        for pair in range(2):
+            for s in range(PASSES):
+                for f in (2 * pair, 2 * pair + 1):
+                    cols = slice(f * D, (f + 1) * D)
+                    nc.tensor.matmul_mx(
+                        out=pre[f][:],
+                        lhsT=a_words[s][:, cols].bitcast(FP8X4), lhsT_scale=a_scales[s][:, cols],
+                        rhs=wa_sb[pair][:, (f % 2) * PASSES + s, :].bitcast(FP4X4), rhs_scale=wa_sc[:, f * PASSES + s, :],
+                        start=(s == 0), stop=(s == PASSES - 1))
+
+        h_bf = [sb(f"h_bf{pair}", [P, 4 * 256], BF16, at=4096 * pair) for pair in range(2)]
+        h_rows = [sb(f"h_rows{f}", [P, H], BF16) for f in range(F)]
+        for pair in range(2):
+            turned = psum.tile([P, 2, 2, D], F32, name=f"turned{pair}", tag="turn", bufs=2)
+            for g in range(2):
+                f = 2 * pair + g
+                nc.scalar.activation(
+                    out=h_rows[f][:].rearrange("m (u p e) -> m u p e", u=2, e=2),
+                    in_=pre[f][:].rearrange("m (p u e) -> m u p e", u=2, e=2), func=ACT.Silu)
+                for u in range(2):
+                    nc.tensor.transpose(turned[:, g, u, :], h_rows[f][:].bitcast(F32)[:, u * P : (u + 1) * P], ident[:])
+            nc.scalar.copy(
+                out=h_bf[pair][:].bitcast(F32).rearrange("p (g m u) -> p g m u", g=2, u=2),
+                in_=turned[:].rearrange("p g u m -> p g m u"))
+
+        gate_ps = psum.tile([P, P], F32, name="gate_ps", tag="turn", bufs=2)
+        nc.tensor.transpose(gate_ps[:], gate_rows[:], ident[:])
+        gate_cols = sb("gate_cols", [P, 8], F32)
+        nc.scalar.copy(out=gate_cols[:], in_=gate_ps[:, 0:8])
+
+        y_sb = sb("y_sb", [P, E * C], F32)
+
+        def gather_slots(name, window, first, count, dtype, at=None):
+            gathered = sb(name, [P, count], dtype, at=at)
+            nc.vector.tensor_copy(gathered[:], window.indirect(offs_sb[:, first // 16 : (first + count) // 16]))
+            return gathered
+
+        def experts(first, count, words, scales):
+            y_ps = psum.tile([P, count * C], F32, name=f"y_ps{first}", tag="y", bufs=2)
+            for e in range(first, first + count):
+                for s in range(PASSES):
+                    tile, base = words[s]
+                    nc.tensor.matmul_mx(
+                        out=y_ps[:, (e - first) * C : (e - first + 1) * C],
+                        lhsT=w_sb[e // 4][:, (e % 4) * PASSES + s, :].bitcast(FP8X4), lhsT_scale=w_sc[:, e * PASSES + s, :],
+                        rhs=tile[:, (e - base) * C : (e - base + 1) * C].bitcast(FP8X4),
+                        rhs_scale=scales[4 * s : P, (e % 4) * C : (e % 4 + 1) * C],
+                        start=(s == 0), stop=(s == PASSES - 1))
+            nc.scalar.copy(out=y_sb[:, first * C : (first + count) * C], in_=y_ps[:])
+
+        def second_layer(pair):
+            h_codes = sb(f"h_codes{pair}", [P, 256], U32)
+            h_scales = sb(f"h_scales{pair}", [P, 256], U8)
+            nc.vector.quantize_mx(out=h_codes[:].bitcast(FP8X4), scales=h_scales[:], in_=h_bf[pair][:])
+            z_ps = psum.tile([P, 256], F32, name=f"z_ps{pair}", tag="wide", bufs=4)
+            for g in range(2):
+                f = 2 * pair + g
+                cols = slice(g * D, (g + 1) * D)
+                nc.tensor.matmul_mx(
+                    out=z_ps[:, cols], lhsT=wb_sb[:, f, :].bitcast(FP4X4), lhsT_scale=wb_sc[:, f, :],
+                    rhs=h_codes[:, cols].bitcast(FP8X4), rhs_scale=h_scales[:, cols], start=True, stop=True)
+            return z_ps
+
+
+        def scatter(adapted, pair, z_ps, tag, at=None):
+            z_sb = sb(f"z_sb{pair}", [P, 256], F32, tag, at)
+            nc.scalar.copy(out=z_sb[:], in_=z_ps[:])
+            nc.vector.tensor_tensor(adapted[:].indirect(offs2_sb[:, pair * 16 : (pair + 1) * 16]),
+                                    z_sb[:], gate2_sb[:, pair * 256 : (pair + 1) * 256], ALU.mult)
+
+        xw = [x_sb[s][:].bitcast(U32) for s in range(PASSES)]
+        w00 = gather_slots("w00", xw[0], 0, HALF, U32)
+        w01 = gather_slots("w01", xw[1], 0, HALF, U32)
+        s0 = gather_slots("s0", xs_packed[:], 0, HALF, U8)
+        experts(0, 4, [(w00, 0), (w01, 0)], s0)
+        z0 = second_layer(0)
+        s1 = gather_slots("s1", xs_packed[:], HALF, HALF, U8, at=0)
+        w10 = gather_slots("w10", xw[0], HALF, HALF, U32, at=1024)
+        z1 = second_layer(1)
+        w11a = gather_slots("w11a", xw[1], HALF, 256, U32, at=4096)
+        experts(4, 2, [(w10, 4), (w11a, 4)], s1)
+        w11b = gather_slots("w11b", xw[1], HALF + 256, 256, U32, at=5120)
+        experts(6, 2, [(w10, 4), (w11b, 6)], s1)
+        adapted = sb("adapted", [P, T], F32, "x_sb1")
+        scatter(adapted, 0, z0, "picked0")
+
+        def gated_choice(r, first, count):
+            name = f"{r}_{first}"
+            picked = sb(f"picked{r}" if r == 0 else f"picked{name}", [P, count * P], F32)
+            nc.vector.tensor_copy(picked[:], y_sb[:].indirect(pos_sb[r][:, first * 8 : (first + count) * 8]))
+            by_token = psum.tile([P, count, N], F32, name=f"by_token{name}", tag="wide", bufs=4)
+            scaled = sb(f"scaled{name}", [P, count, N], F32)
+            for c in range(count):
+                nc.tensor.transpose(by_token[:, c, :], picked[:, c * P : (c + 1) * P], ident[:])
+            for c in range(count):
+                col = 4 * r + first + c
+                nc.scalar.activation(out=scaled[:, c, :], in_=by_token[:, c, :], func=ACT.Copy,
+                                     scale=gate_cols[:, col : col + 1])
+            return [scaled[:, c, :] for c in range(count)]
+
+        gated = [gated_choice(0, 0, 4), gated_choice(1, 0, 2) + gated_choice(1, 2, 2)]
+        scatter(adapted, 1, z1, None, at=5120)
+        for half in range(2):
+            o_ps = psum.tile([P, 256], F32, name=f"o_ps{half}", tag="y", bufs=2)
+            for g in range(2):
+                for r in range(2):
+                    nc.tensor.matmul(o_ps[:, g * P : (g + 1) * P], gated[r][2 * half + g], ident[:],
+                                     is_transpose=True, start=(r == 0), stop=(r == 1))
+            cols = slice(half * 256, (half + 1) * 256)
+            result = sb(f"result{half}", [P, 256], F32)
+            nc.vector.tensor_tensor(result[:], o_ps[:], adapted[:, cols], ALU.add)
+            nc.sync.dma_start(out=out[:, cols], in_=result[:])

@@ -43,8 +43,7 @@ def tile_moe_mlr_silu_kernel(
         offs2_sb = keep.tile([P, T // 16], U16, name="offs2_sb")
         pos_sb = [keep.tile([P, T // 16], U16, name=f"pos{r}_sb") for r in (1, 2)]
 
-        x_sb = [sb(f"x_sb{s}", [P, WINDOW], I32) for s in range(PASSES)]
-        xs_apart = sb("xs_apart", [P, T + WINDOW], U8)
+        x_sb = [sb("x_sb0", [P, WINDOW], I32), sb("x_sb1", [P, WINDOW], I32, at=0)]
         xs_packed = sb("xs_packed", [P, WINDOW], U8)
         wa_sb = [sb(f"wa_sb{h}", [P, 4, 2 * H], U8) for h in range(2)]
         wa_sc = sb("wa_sc", [P, F * PASSES, H], U8)
@@ -56,14 +55,15 @@ def tile_moe_mlr_silu_kernel(
         gate2_sb = sb("gate2_sb", [P, T], F32)
         ident = sb("ident", [P, P], F32)
 
-        nc.vector.memset(xs_apart[:].bitcast(I32), 0)
+        nc.vector.memset(xs_packed[:].bitcast(I32), 0)
         for s in range(PASSES):
             nc.vector.memset(x_sb[s][:, T:WINDOW], 0)
-        nc.gpsimd.memset(wa_sc[:].rearrange("p a i -> p (a i)").bitcast(I32), 0)
-        nc.vector.memset(xs_packed[:].bitcast(I32), 0)
-        nc.gpsimd.memset(w_sc[:].rearrange("p a i -> p (a i)").bitcast(I32), 0)
-        nc.gpsimd.memset(wb_sc[:].rearrange("p a i -> p (a i)").bitcast(I32), 0)
-        nc.gpsimd.memset(gate_rows[:], 0.0)
+        nc.vector.memset(wa_sc[:].rearrange("p a i -> p (a i)").bitcast(I32), 0)
+        a_scales = [sb(f"a_scales{s}", [P, T], U8) for s in range(PASSES)]
+        nc.vector.memset(a_scales[1][:].bitcast(I32), 0)
+        nc.vector.memset(w_sc[:].rearrange("p a i -> p (a i)").bitcast(I32), 0)
+        nc.vector.memset(wb_sc[:].rearrange("p a i -> p (a i)").bitcast(I32), 0)
+        nc.vector.memset(gate_rows[:], 0.0)
         make_identity(nc, ident[:])
 
         def load_scale_rows(plane, rows):
@@ -76,16 +76,14 @@ def tile_moe_mlr_silu_kernel(
 
         nc.sync.dma_start(offs2_sb[:], offs2)
         nc.sync.dma_start(out=x_sb[0][:, 0:T], in_=x_view[0])
-        load_scale_rows(xs_apart[:, 0 : PASSES * T].rearrange("p (s t) -> p s t", s=PASSES),
-                        x_scales.rearrange("s (q j) t -> j q s t", j=4))
+        for q in range(4):
+            nc.sync.dma_start(out=xs_packed[32 * q : 32 * q + 8, 0:T].bitcast(I32),
+                              in_=x_scales[:, 4 * q : 4 * q + 4, :].bitcast(I32))
         nc.sync.dma_start(out=x_sb[1][:, 0:T], in_=x_view[1])
         nc.sync.dma_start(out=wa_sb[0][:].bitcast(I32), in_=wa_view[:, 0:4, :])
         load_scale_rows(wa_sc[:], wa_scales.rearrange("f s (q j) i -> j q (f s) i", j=4))
         nc.sync.dma_start(offs_sb[:], offs)
         nc.sync.dma_start(out=wa_sb[1][:].bitcast(I32), in_=wa_view[:, 4:8, :])
-        for q in range(4):
-            nc.sync.dma_start(out=xs_packed[32 * q : 32 * q + 8, 0:T].bitcast(I32),
-                              in_=x_scales[:, 4 * q : 4 * q + 4, :].bitcast(I32))
         nc.sync.dma_start(out=wb_sb[:].bitcast(I32), in_=wb_words.rearrange("f s p b -> p (f s) b").bitcast(I32))
         load_scale_rows(wb_sc[:], wb_scales.rearrange("f s (q j) n -> j q (f s) n", j=4))
         nc.sync.dma_start(out=gate2_sb[:], in_=gate2)
@@ -97,9 +95,9 @@ def tile_moe_mlr_silu_kernel(
         nc.sync.dma_start(pos_sb[1][:], pos2)
 
         a_words = [sb(f"a_words{s}", [P, T], U32) for s in range(PASSES)]
-        a_scales = [sb(f"a_scales{s}", [P, T], U8) for s in range(PASSES)]
+        nc.vector.tensor_copy(a_scales[0][:], xs_packed[:].indirect(offs2_sb[:]))
+        nc.sync.dma_start(out=a_scales[1][0:112, :].bitcast(I32), in_=a_scales[0][4:116, :].bitcast(I32))
         for s in range(PASSES):
-            nc.vector.tensor_copy(a_scales[s][:], xs_apart[:, s * T : s * T + WINDOW].indirect(offs2_sb[:]))
             nc.vector.tensor_copy(a_words[s][:], x_sb[s][:].bitcast(U32).indirect(offs2_sb[:]))
 
         pre = [psum.tile([P, H], F32, name=f"pre{f}", tag="wide", bufs=4) for f in range(F)]
@@ -113,7 +111,7 @@ def tile_moe_mlr_silu_kernel(
                         rhs=wa_sb[pair][:, (f % 2) * PASSES + s, :].bitcast(FP4X4), rhs_scale=wa_sc[:, f * PASSES + s, :],
                         start=(s == 0), stop=(s == PASSES - 1))
 
-        h_bf = [sb(f"h_bf{pair}", [P, 4 * 256], BF16, at=4096 * pair) for pair in range(2)]
+        h_bf = [sb(f"h_bf{pair}", [P, 4 * 256], BF16, at=(6144, 2816)[pair]) for pair in range(2)]
         h_rows = [sb(f"h_rows{f}", [P, H], BF16) for f in range(F)]
         for pair in range(2):
             turned = psum.tile([P, 2, 2, D], F32, name=f"turned{pair}", tag="turn", bufs=2)
@@ -141,7 +139,7 @@ def tile_moe_mlr_silu_kernel(
             return gathered
 
         def experts(first, count, words, scales):
-            y_ps = psum.tile([P, count * C], F32, name=f"y_ps{first}", tag="y", bufs=2)
+            y_ps = psum.tile([P, count * C], F32, name=f"y_ps{first}", tag="yb" if first == 4 else "ya")
             for e in range(first, first + count):
                 for s in range(PASSES):
                     tile, base = words[s]
@@ -153,11 +151,14 @@ def tile_moe_mlr_silu_kernel(
                         start=(s == 0), stop=(s == PASSES - 1))
             nc.scalar.copy(out=y_sb[:, first * C : (first + count) * C], in_=y_ps[:])
 
-        def second_layer(pair):
+        def quantise(pair):
             h_codes = sb(f"h_codes{pair}", [P, 256], U32)
             h_scales = sb(f"h_scales{pair}", [P, 256], U8)
             nc.vector.quantize_mx(out=h_codes[:].bitcast(FP8X4), scales=h_scales[:], in_=h_bf[pair][:])
-            z_ps = psum.tile([P, 256], F32, name=f"z_ps{pair}", tag="wide", bufs=4)
+            return h_codes, h_scales
+
+        def second_layer(pair, h_codes, h_scales):
+            z_ps = psum.tile([P, 256], F32, name=f"z_ps{pair}", **({"tag": "ya"} if pair else {"tag": "wide", "bufs": 4}))
             for g in range(2):
                 f = 2 * pair + g
                 cols = slice(g * D, (g + 1) * D)
@@ -178,20 +179,20 @@ def tile_moe_mlr_silu_kernel(
         w01 = gather_slots("w01", xw[1], 0, HALF, U32)
         s0 = gather_slots("s0", xs_packed[:], 0, HALF, U8)
         experts(0, 4, [(w00, 0), (w01, 0)], s0)
-        z0 = second_layer(0)
-        s1 = gather_slots("s1", xs_packed[:], HALF, HALF, U8, at=0)
-        w10 = gather_slots("w10", xw[0], HALF, HALF, U32, at=1024)
-        z1 = second_layer(1)
-        w11a = gather_slots("w11a", xw[1], HALF, 256, U32, at=4096)
+        s1 = gather_slots("s1", xs_packed[:], HALF, HALF, U8)
+        w10 = gather_slots("w10", xw[0], HALF, HALF, U32)
+        z0 = second_layer(0, *quantise(0))
+        w11a = gather_slots("w11a", xw[1], HALF, 256, U32, at=6144)
         experts(4, 2, [(w10, 4), (w11a, 4)], s1)
-        w11b = gather_slots("w11b", xw[1], HALF + 256, 256, U32, at=5120)
+        w11b = gather_slots("w11b", xw[1], HALF + 256, 256, U32, at=7168)
         experts(6, 2, [(w10, 4), (w11b, 6)], s1)
-        adapted = sb("adapted", [P, T], F32, "x_sb1")
-        scatter(adapted, 0, z0, "picked0")
+        z1 = second_layer(1, *quantise(1))
+        adapted = sb("adapted", [P, T], F32, at=1792)
+        scatter(adapted, 0, z0, None, at=4864)
 
         def gated_choice(r, first, count):
             name = f"{r}_{first}"
-            picked = sb(f"picked{r}" if r == 0 else f"picked{name}", [P, count * P], F32)
+            picked = sb(f"picked{name}", [P, count * P], F32, at=3840 if r == 0 else None)
             nc.vector.tensor_copy(picked[:], y_sb[:].indirect(pos_sb[r][:, first * 8 : (first + count) * 8]))
             by_token = psum.tile([P, count, N], F32, name=f"by_token{name}", tag="wide", bufs=4)
             scaled = sb(f"scaled{name}", [P, count, N], F32)
@@ -204,9 +205,9 @@ def tile_moe_mlr_silu_kernel(
             return [scaled[:, c, :] for c in range(count)]
 
         gated = [gated_choice(0, 0, 4), gated_choice(1, 0, 2) + gated_choice(1, 2, 2)]
-        scatter(adapted, 1, z1, None, at=5120)
+        scatter(adapted, 1, z1, None)
         for half in range(2):
-            o_ps = psum.tile([P, 256], F32, name=f"o_ps{half}", tag="y", bufs=2)
+            o_ps = psum.tile([P, 256], F32, name=f"o_ps{half}", tag=("yb", "ya")[half])
             for g in range(2):
                 for r in range(2):
                     nc.tensor.matmul(o_ps[:, g * P : (g + 1) * P], gated[r][2 * half + g], ident[:],

@@ -61,9 +61,9 @@ def tile_moe_mlr_silu_kernel(
         nc.vector.memset(wa_sc[:].rearrange("p a i -> p (a i)").bitcast(I32), 0)
         a_scales = [sb(f"a_scales{s}", [P, T], U8) for s in range(PASSES)]
         nc.vector.memset(a_scales[1][:].bitcast(I32), 0)
-        nc.vector.memset(w_sc[:].rearrange("p a i -> p (a i)").bitcast(I32), 0)
-        nc.vector.memset(wb_sc[:].rearrange("p a i -> p (a i)").bitcast(I32), 0)
-        nc.vector.memset(gate_rows[:], 0.0)
+        nc.gpsimd.memset(w_sc[:].rearrange("p a i -> p (a i)").bitcast(I32), 0)
+        nc.gpsimd.memset(wb_sc[:].rearrange("p a i -> p (a i)").bitcast(I32), 0)
+        nc.gpsimd.memset(gate_rows[:], 0.0)
         make_identity(nc, ident[:])
 
         def load_scale_rows(plane, rows):
@@ -75,10 +75,11 @@ def tile_moe_mlr_silu_kernel(
         w_view = w_words.rearrange("e s p n d -> p (e s) (n d)").bitcast(I32)
 
         nc.sync.dma_start(offs2_sb[:], offs2)
-        nc.sync.dma_start(out=x_sb[0][:, 0:T], in_=x_view[0])
+        nc.sync.dma_start(pos_sb[0][:], pos1)
         for q in range(4):
             nc.sync.dma_start(out=xs_packed[32 * q : 32 * q + 8, 0:T].bitcast(I32),
                               in_=x_scales[:, 4 * q : 4 * q + 4, :].bitcast(I32))
+        nc.sync.dma_start(out=x_sb[0][:, 0:T], in_=x_view[0])
         nc.sync.dma_start(out=x_sb[1][:, 0:T], in_=x_view[1])
         nc.sync.dma_start(out=wa_sb[0][:].bitcast(I32), in_=wa_view[:, 0:4, :])
         load_scale_rows(wa_sc[:], wa_scales.rearrange("f s (q j) i -> j q (f s) i", j=4))
@@ -91,12 +92,11 @@ def tile_moe_mlr_silu_kernel(
         load_scale_rows(w_sc[:], w_scales.rearrange("e s (q j) n -> j q (e s) n", j=4))
         nc.sync.dma_start(out=w_sb[1][:], in_=w_view[:, 8:16, :])
         nc.sync.dma_start(out=gate_rows[0:8, :], in_=gate[:, 0, :].rearrange("r (c t) -> r c t", t=P))
-        nc.sync.dma_start(pos_sb[0][:], pos1)
         nc.sync.dma_start(pos_sb[1][:], pos2)
 
         a_words = [sb(f"a_words{s}", [P, T], U32) for s in range(PASSES)]
         nc.vector.tensor_copy(a_scales[0][:], xs_packed[:].indirect(offs2_sb[:]))
-        nc.sync.dma_start(out=a_scales[1][0:112, :].bitcast(I32), in_=a_scales[0][4:116, :].bitcast(I32))
+        nc.scalar.dma_start(out=a_scales[1][0:112, :].bitcast(I32), in_=a_scales[0][4:116, :].bitcast(I32))
         for s in range(PASSES):
             nc.vector.tensor_copy(a_words[s][:], x_sb[s][:].bitcast(U32).indirect(offs2_sb[:]))
 

@@ -18,9 +18,24 @@ ACT = mybir.ActivationFunctionType
 ALU = mybir.AluOpType
 
 P = 128
-PASSES = 2
+PASSES = K // 512
+CHOICES = 2
+LIST_ROWS = 16
+QUADRANT = 32
+SCALE_ROWS = 4
+MOVED_ROWS = 112
 WINDOW = 704
-HALF = 512
+PAIR = 2
+PAIR_SLOTS = PAIR * D
+TOKEN_BLOCKS = T // P
+HALF_BLOCKS = TOKEN_BLOCKS // 2
+
+AT_X1 = 0
+AT_H1 = AT_X1 + 4 * WINDOW
+AT_Z0 = AT_H1 + 8 * PAIR_SLOTS
+AT_CHOICE0 = AT_Z0 - 4 * PAIR_SLOTS
+AT_ADAPTED = AT_CHOICE0 - 4 * T
+AT_H0 = 6144
 
 
 def tile_moe_mlr_silu_kernel(
@@ -31,188 +46,201 @@ def tile_moe_mlr_silu_kernel(
     with ExitStack() as ctx:
         keep = ctx.enter_context(tc.tile_pool(name="keep", bufs=1))
         psum = ctx.enter_context(tc.psum_pool(name="psum", bufs=1))
+        shared = ctx.enter_context(tc.tile_pool(name="shared", bufs=1))
 
-        reuse = ctx.enter_context(tc.tile_pool(name="reuse", bufs=1))
+        def sbuf(name, shape, dtype, at=None):
+            if at is None:
+                return keep.tile(shape, dtype, name=name, align_bytes=64)
+            return shared.tile(shape, dtype, name=name, offset=at, align_bytes=64)
 
-        def sb(name, shape, dtype, tag=None, at=None):
-            if at is not None:
-                return reuse.tile(shape, dtype, name=name, offset=at, align_bytes=64)
-            return keep.tile(shape, dtype, name=name, tag=tag or name, align_bytes=64)
+        def ring_bank(name, shape):
+            return psum.tile(shape, F32, name=name, tag="ring", bufs=4)
 
-        offs_sb = keep.tile([P, E * C // 16], U16, name="offs_sb")
-        offs2_sb = keep.tile([P, T // 16], U16, name="offs2_sb")
-        pos_sb = [keep.tile([P, T // 16], U16, name=f"pos{r}_sb") for r in (1, 2)]
+        def turn_bank(name, shape):
+            return psum.tile(shape, F32, name=name, tag="turn", bufs=2)
 
-        x_sb = [sb("x_sb0", [P, WINDOW], I32), sb("x_sb1", [P, WINDOW], I32, at=0)]
-        xs_packed = sb("xs_packed", [P, WINDOW], U8)
-        wa_sb = [sb(f"wa_sb{h}", [P, 4, 2 * H], U8) for h in range(2)]
-        wa_sc = sb("wa_sc", [P, F * PASSES, H], U8)
-        w_sb = [sb(f"w_sb{h}", [P, 8, N], I32) for h in range(2)]
-        w_sc = sb("w_sc", [P, E * PASSES, N], U8)
-        wb_sb = sb("wb_sb", [P, F, 2 * N], U8)
-        wb_sc = sb("wb_sc", [P, F, N], U8)
-        gate_rows = sb("gate_rows", [P, P], F32)
-        gate2_sb = sb("gate2_sb", [P, T], F32)
-        ident = sb("ident", [P, P], F32)
+        def own_bank(name, shape, tag):
+            return psum.tile(shape, F32, name=name, tag=tag)
 
-        nc.vector.memset(xs_packed[:].bitcast(I32), 0)
+        def entries(list_sb, first, count):
+            return list_sb[:, first // LIST_ROWS : (first + count) // LIST_ROWS]
+
+        offs_sb = keep.tile([P, E * C // LIST_ROWS], U16, name="offs_sb")
+        offs2_sb = keep.tile([P, F * D // LIST_ROWS], U16, name="offs2_sb")
+        pos_sb = [keep.tile([P, T // LIST_ROWS], U16, name=f"pos_sb{r}") for r in range(CHOICES)]
+
+        x_sb = [sbuf("x_sb0", [P, WINDOW], I32), sbuf("x_sb1", [P, WINDOW], I32, at=AT_X1)]
+        x_plane = sbuf("x_plane", [P, WINDOW], U8)
+        wa_sb = [sbuf(f"wa_sb{pair}", [P, PAIR * PASSES, 2 * H], U8) for pair in range(F // PAIR)]
+        wa_plane = sbuf("wa_plane", [P, F * PASSES, H], U8)
+        w_sb = [sbuf(f"w_sb{half}", [P, E // 2 * PASSES, N], I32) for half in range(2)]
+        w_plane = sbuf("w_plane", [P, E * PASSES, N], U8)
+        wb_sb = sbuf("wb_sb", [P, F, 2 * N], U8)
+        wb_plane = sbuf("wb_plane", [P, F, N], U8)
+        gate_rows = sbuf("gate_rows", [P, P], F32)
+        gate2_sb = sbuf("gate2_sb", [P, F * D], F32)
+        ident = sbuf("ident", [P, P], F32)
+        a_planes = [sbuf(f"a_plane{s}", [P, F * D], U8) for s in range(PASSES)]
+
+        nc.vector.memset(x_plane[:].bitcast(I32), 0)
         for s in range(PASSES):
             nc.vector.memset(x_sb[s][:, T:WINDOW], 0)
-        nc.vector.memset(wa_sc[:].rearrange("p a i -> p (a i)").bitcast(I32), 0)
-        a_scales = [sb(f"a_scales{s}", [P, T], U8) for s in range(PASSES)]
-        nc.vector.memset(a_scales[1][:].bitcast(I32), 0)
-        nc.gpsimd.memset(w_sc[:].rearrange("p a i -> p (a i)").bitcast(I32), 0)
-        nc.gpsimd.memset(wb_sc[:].rearrange("p a i -> p (a i)").bitcast(I32), 0)
-        nc.gpsimd.memset(gate_rows[:], 0.0)
+        nc.vector.memset(wa_plane[:].rearrange("p a i -> p (a i)").bitcast(I32), 0)
+        nc.vector.memset(a_planes[1][:].bitcast(I32), 0)
+        nc.vector.memset(w_plane[:].rearrange("p a n -> p (a n)").bitcast(I32), 0)
+        nc.vector.memset(wb_plane[:].rearrange("p a n -> p (a n)").bitcast(I32), 0)
+        nc.vector.memset(gate_rows[:], 0.0)
         make_identity(nc, ident[:])
 
-        def load_scale_rows(plane, rows):
-            for j in range(4):
-                nc.sync.dma_start(out=plane[j:P:32].bitcast(I32), in_=rows[j].bitcast(I32))
+        def load_plane(plane, scales):
+            rows = scales.rearrange("m s (q j) c -> j q (m s) c", j=SCALE_ROWS)
+            for j in range(SCALE_ROWS):
+                nc.sync.dma_start(out=plane[j:P:QUADRANT].bitcast(I32), in_=rows[j].bitcast(I32))
 
         x_view = x_words.rearrange("s p t d -> s p (t d)").bitcast(I32)
         wa_view = wa_words.rearrange("f s p b -> p (f s) b").bitcast(I32)
         w_view = w_words.rearrange("e s p n d -> p (e s) (n d)").bitcast(I32)
-
         nc.sync.dma_start(offs2_sb[:], offs2)
         nc.sync.dma_start(pos_sb[0][:], pos1)
-        for q in range(4):
-            nc.sync.dma_start(out=xs_packed[32 * q : 32 * q + 8, 0:T].bitcast(I32),
-                              in_=x_scales[:, 4 * q : 4 * q + 4, :].bitcast(I32))
-        nc.sync.dma_start(out=x_sb[0][:, 0:T], in_=x_view[0])
-        nc.sync.dma_start(out=x_sb[1][:, 0:T], in_=x_view[1])
-        nc.sync.dma_start(out=wa_sb[0][:].bitcast(I32), in_=wa_view[:, 0:4, :])
-        load_scale_rows(wa_sc[:], wa_scales.rearrange("f s (q j) i -> j q (f s) i", j=4))
+        for q in range(P // QUADRANT):
+            nc.sync.dma_start(
+                out=x_plane[QUADRANT * q : QUADRANT * q + PASSES * SCALE_ROWS, 0:T].bitcast(I32),
+                in_=x_scales[:, SCALE_ROWS * q : SCALE_ROWS * (q + 1), :].bitcast(I32))
+        for s in range(PASSES):
+            nc.sync.dma_start(out=x_sb[s][:, 0:T], in_=x_view[s])
+        nc.sync.dma_start(out=wa_sb[0][:].bitcast(I32), in_=wa_view[:, 0 : PAIR * PASSES, :])
+        load_plane(wa_plane[:], wa_scales)
         nc.sync.dma_start(offs_sb[:], offs)
-        nc.sync.dma_start(out=wa_sb[1][:].bitcast(I32), in_=wa_view[:, 4:8, :])
+        nc.sync.dma_start(out=wa_sb[1][:].bitcast(I32), in_=wa_view[:, PAIR * PASSES : F * PASSES, :])
         nc.sync.dma_start(out=wb_sb[:].bitcast(I32), in_=wb_words.rearrange("f s p b -> p (f s) b").bitcast(I32))
-        load_scale_rows(wb_sc[:], wb_scales.rearrange("f s (q j) n -> j q (f s) n", j=4))
+        load_plane(wb_plane[:], wb_scales)
+        nc.sync.dma_start(out=gate_rows[0 : CHOICES * TOKEN_BLOCKS, :],
+                          in_=gate[:, 0, :].rearrange("r (c t) -> r c t", t=P))
+        nc.sync.dma_start(out=w_sb[0][:], in_=w_view[:, 0 : E // 2 * PASSES, :])
+        load_plane(w_plane[:], w_scales)
+        nc.sync.dma_start(out=w_sb[1][:], in_=w_view[:, E // 2 * PASSES : E * PASSES, :])
         nc.sync.dma_start(out=gate2_sb[:], in_=gate2)
-        nc.sync.dma_start(out=w_sb[0][:], in_=w_view[:, 0:8, :])
-        load_scale_rows(w_sc[:], w_scales.rearrange("e s (q j) n -> j q (e s) n", j=4))
-        nc.sync.dma_start(out=w_sb[1][:], in_=w_view[:, 8:16, :])
-        nc.sync.dma_start(out=gate_rows[0:8, :], in_=gate[:, 0, :].rearrange("r (c t) -> r c t", t=P))
         nc.sync.dma_start(pos_sb[1][:], pos2)
 
-        a_words = [sb(f"a_words{s}", [P, T], U32) for s in range(PASSES)]
-        nc.vector.tensor_copy(a_scales[0][:], xs_packed[:].indirect(offs2_sb[:]))
-        nc.scalar.dma_start(out=a_scales[1][0:112, :].bitcast(I32), in_=a_scales[0][4:116, :].bitcast(I32))
+        x_windows = [x_sb[s][:].bitcast(U32) for s in range(PASSES)]
+        a_words = [sbuf(f"a_words{s}", [P, F * D], U32) for s in range(PASSES)]
+        nc.vector.tensor_copy(a_planes[0][:], x_plane[:].indirect(offs2_sb[:]))
+        nc.scalar.dma_start(out=a_planes[1][0:MOVED_ROWS, :].bitcast(I32),
+                            in_=a_planes[0][SCALE_ROWS : SCALE_ROWS + MOVED_ROWS, :].bitcast(I32))
         for s in range(PASSES):
-            nc.vector.tensor_copy(a_words[s][:], x_sb[s][:].bitcast(U32).indirect(offs2_sb[:]))
+            nc.vector.tensor_copy(a_words[s][:], x_windows[s].indirect(offs2_sb[:]))
 
-        pre = [psum.tile([P, H], F32, name=f"pre{f}", tag="wide", bufs=4) for f in range(F)]
-        for pair in range(2):
+        pre = [ring_bank(f"pre{f}", [P, H]) for f in range(F - 1)] + [own_bank("pre_last", [P, H], "late")]
+        for pair in range(F // PAIR):
             for s in range(PASSES):
-                for f in (2 * pair, 2 * pair + 1):
-                    cols = slice(f * D, (f + 1) * D)
+                for g in range(PAIR):
+                    f = PAIR * pair + g
+                    slots = slice(f * D, (f + 1) * D)
                     nc.tensor.matmul_mx(
                         out=pre[f][:],
-                        lhsT=a_words[s][:, cols].bitcast(FP8X4), lhsT_scale=a_scales[s][:, cols],
-                        rhs=wa_sb[pair][:, (f % 2) * PASSES + s, :].bitcast(FP4X4), rhs_scale=wa_sc[:, f * PASSES + s, :],
+                        lhsT=a_words[s][:, slots].bitcast(FP8X4), lhsT_scale=a_planes[s][:, slots],
+                        rhs=wa_sb[pair][:, g * PASSES + s, :].bitcast(FP4X4), rhs_scale=wa_plane[:, f * PASSES + s, :],
                         start=(s == 0), stop=(s == PASSES - 1))
 
-        h_bf = [sb(f"h_bf{pair}", [P, 4 * 256], BF16, at=(6144, 2816)[pair]) for pair in range(2)]
-        h_rows = [sb(f"h_rows{f}", [P, H], BF16) for f in range(F)]
-        for pair in range(2):
-            turned = psum.tile([P, 2, 2, D], F32, name=f"turned{pair}", tag="turn", bufs=2)
-            for g in range(2):
-                f = 2 * pair + g
+        h_bf = [sbuf(f"h_bf{pair}", [P, 4 * PAIR_SLOTS], BF16, at=at) for pair, at in enumerate((AT_H0, AT_H1))]
+        h_rows = [sbuf(f"h_rows{f}", [P, H], BF16) for f in range(F)]
+        for pair in range(F // PAIR):
+            turned = turn_bank(f"turned{pair}", [P, PAIR, 2, D])
+            for g in range(PAIR):
+                f = PAIR * pair + g
                 nc.scalar.activation(
                     out=h_rows[f][:].rearrange("m (u p e) -> m u p e", u=2, e=2),
                     in_=pre[f][:].rearrange("m (p u e) -> m u p e", u=2, e=2), func=ACT.Silu)
                 for u in range(2):
                     nc.tensor.transpose(turned[:, g, u, :], h_rows[f][:].bitcast(F32)[:, u * P : (u + 1) * P], ident[:])
             nc.scalar.copy(
-                out=h_bf[pair][:].bitcast(F32).rearrange("p (g m u) -> p g m u", g=2, u=2),
+                out=h_bf[pair][:].bitcast(F32).rearrange("p (g m u) -> p g m u", g=PAIR, u=2),
                 in_=turned[:].rearrange("p g u m -> p g m u"))
 
-        gate_ps = psum.tile([P, P], F32, name="gate_ps", tag="turn", bufs=2)
-        nc.tensor.transpose(gate_ps[:], gate_rows[:], ident[:])
-        gate_cols = sb("gate_cols", [P, 8], F32)
-        nc.scalar.copy(out=gate_cols[:], in_=gate_ps[:, 0:8])
+        gate_turned = turn_bank("gate_turned", [P, P])
+        nc.tensor.transpose(gate_turned[:], gate_rows[:], ident[:])
+        gate_cols = sbuf("gate_cols", [P, CHOICES * TOKEN_BLOCKS], F32)
+        nc.scalar.copy(out=gate_cols[:], in_=gate_turned[:, 0 : CHOICES * TOKEN_BLOCKS])
 
-        y_sb = sb("y_sb", [P, E * C], F32)
+        y_sb = sbuf("y_sb", [P, E * C], F32)
 
         def gather_slots(name, window, first, count, dtype, at=None):
-            gathered = sb(name, [P, count], dtype, at=at)
-            nc.vector.tensor_copy(gathered[:], window.indirect(offs_sb[:, first // 16 : (first + count) // 16]))
+            gathered = sbuf(name, [P, count * C], dtype, at=at)
+            nc.vector.tensor_copy(gathered[:], window.indirect(entries(offs_sb, first * C, count * C)))
             return gathered
 
-        def experts(first, count, words, scales):
-            y_ps = psum.tile([P, count * C], F32, name=f"y_ps{first}", tag="yb" if first == 4 else "ya")
-            for e in range(first, first + count):
+        def experts(first, count, words, plane, tag):
+            y_ps = own_bank(f"y_ps{first}", [P, count * C], tag)
+            for g in range(count):
+                half, place = divmod(first + g, E // 2)
+                slots = slice(g * C, (g + 1) * C)
                 for s in range(PASSES):
-                    tile, base = words[s]
                     nc.tensor.matmul_mx(
-                        out=y_ps[:, (e - first) * C : (e - first + 1) * C],
-                        lhsT=w_sb[e // 4][:, (e % 4) * PASSES + s, :].bitcast(FP8X4), lhsT_scale=w_sc[:, e * PASSES + s, :],
-                        rhs=tile[:, (e - base) * C : (e - base + 1) * C].bitcast(FP8X4),
-                        rhs_scale=scales[4 * s : P, (e % 4) * C : (e % 4 + 1) * C],
+                        out=y_ps[:, slots],
+                        lhsT=w_sb[half][:, place * PASSES + s, :].bitcast(FP8X4),
+                        lhsT_scale=w_plane[:, (first + g) * PASSES + s, :],
+                        rhs=words[s][:, slots].bitcast(FP8X4),
+                        rhs_scale=plane[SCALE_ROWS * s : P, place * C : (place + 1) * C],
                         start=(s == 0), stop=(s == PASSES - 1))
             nc.scalar.copy(out=y_sb[:, first * C : (first + count) * C], in_=y_ps[:])
 
-        def quantise(pair):
-            h_codes = sb(f"h_codes{pair}", [P, 256], U32)
-            h_scales = sb(f"h_scales{pair}", [P, 256], U8)
-            nc.vector.quantize_mx(out=h_codes[:].bitcast(FP8X4), scales=h_scales[:], in_=h_bf[pair][:])
-            return h_codes, h_scales
-
-        def second_layer(pair, h_codes, h_scales):
-            z_ps = psum.tile([P, 256], F32, name=f"z_ps{pair}", **({"tag": "ya"} if pair else {"tag": "wide", "bufs": 4}))
-            for g in range(2):
-                f = 2 * pair + g
-                cols = slice(g * D, (g + 1) * D)
+        def second_layer(pair, z_ps, at=None):
+            h_codes = sbuf(f"h_codes{pair}", [P, PAIR_SLOTS], U32)
+            h_plane = sbuf(f"h_plane{pair}", [P, PAIR_SLOTS], U8)
+            nc.vector.quantize_mx(out=h_codes[:].bitcast(FP8X4), scales=h_plane[:], in_=h_bf[pair][:])
+            for g in range(PAIR):
+                f = PAIR * pair + g
+                slots = slice(g * D, (g + 1) * D)
                 nc.tensor.matmul_mx(
-                    out=z_ps[:, cols], lhsT=wb_sb[:, f, :].bitcast(FP4X4), lhsT_scale=wb_sc[:, f, :],
-                    rhs=h_codes[:, cols].bitcast(FP8X4), rhs_scale=h_scales[:, cols], start=True, stop=True)
-            return z_ps
-
-
-        def scatter(adapted, pair, z_ps, tag, at=None):
-            z_sb = sb(f"z_sb{pair}", [P, 256], F32, tag, at)
+                    out=z_ps[:, slots], lhsT=wb_sb[:, f, :].bitcast(FP4X4), lhsT_scale=wb_plane[:, f, :],
+                    rhs=h_codes[:, slots].bitcast(FP8X4), rhs_scale=h_plane[:, slots], start=True, stop=True)
+            z_sb = sbuf(f"z_sb{pair}", [P, PAIR_SLOTS], F32, at=at)
             nc.scalar.copy(out=z_sb[:], in_=z_ps[:])
-            nc.vector.tensor_tensor(adapted[:].indirect(offs2_sb[:, pair * 16 : (pair + 1) * 16]),
-                                    z_sb[:], gate2_sb[:, pair * 256 : (pair + 1) * 256], ALU.mult)
+            return z_sb
 
-        xw = [x_sb[s][:].bitcast(U32) for s in range(PASSES)]
-        w00 = gather_slots("w00", xw[0], 0, HALF, U32)
-        w01 = gather_slots("w01", xw[1], 0, HALF, U32)
-        s0 = gather_slots("s0", xs_packed[:], 0, HALF, U8)
-        experts(0, 4, [(w00, 0), (w01, 0)], s0)
-        s1 = gather_slots("s1", xs_packed[:], HALF, HALF, U8)
-        w10 = gather_slots("w10", xw[0], HALF, HALF, U32)
-        z0 = second_layer(0, *quantise(0))
-        w11a = gather_slots("w11a", xw[1], HALF, 256, U32, at=6144)
-        experts(4, 2, [(w10, 4), (w11a, 4)], s1)
-        w11b = gather_slots("w11b", xw[1], HALF + 256, 256, U32, at=7168)
-        experts(6, 2, [(w10, 4), (w11b, 6)], s1)
-        z1 = second_layer(1, *quantise(1))
-        adapted = sb("adapted", [P, T], F32, at=1792)
-        scatter(adapted, 0, z0, None, at=4864)
+        def scatter(adapted, pair, z_sb):
+            first = pair * PAIR_SLOTS
+            nc.vector.tensor_tensor(adapted[:].indirect(entries(offs2_sb, first, PAIR_SLOTS)),
+                                    z_sb[:], gate2_sb[:, first : first + PAIR_SLOTS], ALU.mult)
 
-        def gated_choice(r, first, count):
-            name = f"{r}_{first}"
-            picked = sb(f"picked{name}", [P, count * P], F32, at=3840 if r == 0 else None)
-            nc.vector.tensor_copy(picked[:], y_sb[:].indirect(pos_sb[r][:, first * 8 : (first + count) * 8]))
-            by_token = psum.tile([P, count, N], F32, name=f"by_token{name}", tag="wide", bufs=4)
-            scaled = sb(f"scaled{name}", [P, count, N], F32)
+        words = [gather_slots(f"words0_{s}", x_windows[s], 0, 4, U32) for s in range(PASSES)]
+        plane = gather_slots("plane0", x_plane[:], 0, E // 2, U8)
+        experts(0, 4, words, plane, "late")
+        plane = gather_slots("plane1", x_plane[:], E // 2, E // 2, U8)
+        words = [gather_slots(f"words4_{s}", x_windows[s], 4, 2, U32) for s in range(PASSES)]
+        experts(4, 2, words, plane, "early")
+        z_first = second_layer(0, ring_bank("z_ps0", [P, PAIR_SLOTS]), at=AT_Z0)
+        words = [gather_slots(f"words6_{s}", x_windows[s], 6, 2, U32, at=AT_H0 + 4 * 2 * C * s) for s in range(PASSES)]
+        experts(6, 2, words, plane, "late")
+        z_second = second_layer(1, own_bank("z_ps1", [P, PAIR_SLOTS], "late"))
+
+        adapted = sbuf("adapted", [P, T], F32, at=AT_ADAPTED)
+        scatter(adapted, 0, z_first)
+
+        def gated_choice(r, first, count, at=None):
+            picked = sbuf(f"picked{r}_{first}", [P, count * P], F32, at=at)
+            nc.vector.tensor_copy(picked[:], y_sb[:].indirect(entries(pos_sb[r], first * P, count * P)))
+            by_token = ring_bank(f"by_token{r}_{first}", [P, count, N])
+            scaled = sbuf(f"scaled{r}_{first}", [P, count, N], F32)
             for c in range(count):
                 nc.tensor.transpose(by_token[:, c, :], picked[:, c * P : (c + 1) * P], ident[:])
             for c in range(count):
-                col = 4 * r + first + c
+                column = r * TOKEN_BLOCKS + first + c
                 nc.scalar.activation(out=scaled[:, c, :], in_=by_token[:, c, :], func=ACT.Copy,
-                                     scale=gate_cols[:, col : col + 1])
+                                     scale=gate_cols[:, column : column + 1])
             return [scaled[:, c, :] for c in range(count)]
 
-        gated = [gated_choice(0, 0, 4), gated_choice(1, 0, 2) + gated_choice(1, 2, 2)]
-        scatter(adapted, 1, z1, None)
-        for half in range(2):
-            o_ps = psum.tile([P, 256], F32, name=f"o_ps{half}", tag=("yb", "ya")[half])
-            for g in range(2):
-                for r in range(2):
-                    nc.tensor.matmul(o_ps[:, g * P : (g + 1) * P], gated[r][2 * half + g], ident[:],
-                                     is_transpose=True, start=(r == 0), stop=(r == 1))
-            cols = slice(half * 256, (half + 1) * 256)
-            result = sb(f"result{half}", [P, 256], F32)
-            nc.vector.tensor_tensor(result[:], o_ps[:], adapted[:, cols], ALU.add)
-            nc.sync.dma_start(out=out[:, cols], in_=result[:])
+        gated = [gated_choice(0, 0, TOKEN_BLOCKS, at=AT_CHOICE0),
+                 gated_choice(1, 0, HALF_BLOCKS) + gated_choice(1, HALF_BLOCKS, HALF_BLOCKS)]
+        scatter(adapted, 1, z_second)
+
+        for half, tag in enumerate(("early", "late")):
+            o_ps = own_bank(f"o_ps{half}", [P, HALF_BLOCKS * P], tag)
+            for c in range(HALF_BLOCKS):
+                for r in range(CHOICES):
+                    nc.tensor.matmul(o_ps[:, c * P : (c + 1) * P], gated[r][HALF_BLOCKS * half + c], ident[:],
+                                     is_transpose=True, start=(r == 0), stop=(r == CHOICES - 1))
+            tokens = slice(half * HALF_BLOCKS * P, (half + 1) * HALF_BLOCKS * P)
+            result = sbuf(f"result{half}", [P, HALF_BLOCKS * P], F32)
+            nc.vector.tensor_tensor(result[:], o_ps[:], adapted[:, tokens], ALU.add)
+            nc.sync.dma_start(out=out[:, tokens], in_=result[:])

@@ -32,8 +32,7 @@ HALF_BLOCKS = TOKEN_BLOCKS // 2
 
 AT_X1 = 0
 AT_H1 = AT_X1 + 4 * WINDOW
-AT_Z0 = AT_H1 + 8 * PAIR_SLOTS
-AT_CHOICE0 = AT_Z0 - 4 * PAIR_SLOTS
+AT_CHOICE0 = AT_H1 + 4 * PAIR_SLOTS
 AT_ADAPTED = AT_CHOICE0 - 4 * T
 AT_H0 = 6144
 
@@ -130,7 +129,7 @@ def tile_moe_mlr_silu_kernel(
         for s in range(PASSES):
             nc.vector.tensor_copy(a_words[s][:], x_windows[s].indirect(offs2_sb[:]))
 
-        pre = [ring_bank(f"pre{f}", [P, H]) for f in range(F - 1)] + [own_bank("pre_last", [P, H], "late")]
+        pre = [ring_bank(f"pre{f}", [P, H]) for f in range(F)]
         for pair in range(F // PAIR):
             for s in range(PASSES):
                 for g in range(PAIR):
@@ -145,7 +144,8 @@ def tile_moe_mlr_silu_kernel(
         h_bf = [sbuf(f"h_bf{pair}", [P, 4 * PAIR_SLOTS], BF16, at=at) for pair, at in enumerate((AT_H0, AT_H1))]
         h_rows = [sbuf(f"h_rows{f}", [P, H], BF16) for f in range(F)]
         for pair in range(F // PAIR):
-            turned = turn_bank(f"turned{pair}", [P, PAIR, 2, D])
+            shape = [P, PAIR, 2, D]
+            turned = turn_bank("turned0", shape) if pair == 0 else own_bank("turned1", shape, "first")
             for g in range(PAIR):
                 f = PAIR * pair + g
                 nc.scalar.activation(
@@ -184,7 +184,7 @@ def tile_moe_mlr_silu_kernel(
                         start=(s == 0), stop=(s == PASSES - 1))
             nc.scalar.copy(out=y_sb[:, first * C : (first + count) * C], in_=y_ps[:])
 
-        def second_layer(pair, z_ps, at=None):
+        def second_layer(pair, z_ps):
             h_codes = sbuf(f"h_codes{pair}", [P, PAIR_SLOTS], U32)
             h_plane = sbuf(f"h_plane{pair}", [P, PAIR_SLOTS], U8)
             nc.vector.quantize_mx(out=h_codes[:].bitcast(FP8X4), scales=h_plane[:], in_=h_bf[pair][:])
@@ -194,7 +194,7 @@ def tile_moe_mlr_silu_kernel(
                 nc.tensor.matmul_mx(
                     out=z_ps[:, slots], lhsT=wb_sb[:, f, :].bitcast(FP4X4), lhsT_scale=wb_plane[:, f, :],
                     rhs=h_codes[:, slots].bitcast(FP8X4), rhs_scale=h_plane[:, slots], start=True, stop=True)
-            z_sb = sbuf(f"z_sb{pair}", [P, PAIR_SLOTS], F32, at=at)
+            z_sb = sbuf(f"z_sb{pair}", [P, PAIR_SLOTS], F32)
             nc.scalar.copy(out=z_sb[:], in_=z_ps[:])
             return z_sb
 
@@ -205,14 +205,14 @@ def tile_moe_mlr_silu_kernel(
 
         words = [gather_slots(f"words0_{s}", x_windows[s], 0, 4, U32) for s in range(PASSES)]
         plane = gather_slots("plane0", x_plane[:], 0, E // 2, U8)
-        experts(0, 4, words, plane, "late")
+        experts(0, 4, words, plane, "first")
         plane = gather_slots("plane1", x_plane[:], E // 2, E // 2, U8)
         words = [gather_slots(f"words4_{s}", x_windows[s], 4, 2, U32) for s in range(PASSES)]
-        experts(4, 2, words, plane, "early")
-        z_first = second_layer(0, ring_bank("z_ps0", [P, PAIR_SLOTS]), at=AT_Z0)
+        experts(4, 2, words, plane, "first")
+        z_first = second_layer(0, ring_bank("z_ps0", [P, PAIR_SLOTS]))
         words = [gather_slots(f"words6_{s}", x_windows[s], 6, 2, U32, at=AT_H0 + 4 * 2 * C * s) for s in range(PASSES)]
-        experts(6, 2, words, plane, "late")
-        z_second = second_layer(1, own_bank("z_ps1", [P, PAIR_SLOTS], "late"))
+        experts(6, 2, words, plane, "second")
+        z_second = second_layer(1, own_bank("z_ps1", [P, PAIR_SLOTS], "second"))
 
         adapted = sbuf("adapted", [P, T], F32, at=AT_ADAPTED)
         scatter(adapted, 0, z_first)
@@ -234,7 +234,7 @@ def tile_moe_mlr_silu_kernel(
                  gated_choice(1, 0, HALF_BLOCKS) + gated_choice(1, HALF_BLOCKS, HALF_BLOCKS)]
         scatter(adapted, 1, z_second)
 
-        for half, tag in enumerate(("early", "late")):
+        for half, tag in enumerate(("first", "second")):
             o_ps = own_bank(f"o_ps{half}", [P, HALF_BLOCKS * P], tag)
             for c in range(HALF_BLOCKS):
                 for r in range(CHOICES):

@@ -24,17 +24,15 @@ LIST_ROWS = 16
 QUADRANT = 32
 SCALE_ROWS = 4
 MOVED_ROWS = 112
-WINDOW = 704
+WINDOW = 688
+PLANE_WINDOW = 1024
 PAIR = 2
 PAIR_SLOTS = PAIR * D
 TOKEN_BLOCKS = T // P
 HALF_BLOCKS = TOKEN_BLOCKS // 2
 
-AT_X1 = 0
-AT_H1 = AT_X1 + 4 * WINDOW
-AT_CHOICE0 = AT_H1 + 4 * PAIR_SLOTS
-AT_ADAPTED = AT_CHOICE0 - 4 * T
-AT_H0 = 6144
+AT_WORDS6 = 0
+AT_GATE_ROWS = 768
 
 
 def tile_moe_mlr_silu_kernel(
@@ -55,9 +53,6 @@ def tile_moe_mlr_silu_kernel(
         def ring_bank(name, shape):
             return psum.tile(shape, F32, name=name, tag="ring", bufs=4)
 
-        def turn_bank(name, shape):
-            return psum.tile(shape, F32, name=name, tag="turn", bufs=2)
-
         def own_bank(name, shape, tag):
             return psum.tile(shape, F32, name=name, tag=tag)
 
@@ -68,60 +63,58 @@ def tile_moe_mlr_silu_kernel(
         offs2_sb = keep.tile([P, F * D // LIST_ROWS], U16, name="offs2_sb")
         pos_sb = [keep.tile([P, T // LIST_ROWS], U16, name=f"pos_sb{r}") for r in range(CHOICES)]
 
-        x_sb = [sbuf("x_sb0", [P, WINDOW], I32), sbuf("x_sb1", [P, WINDOW], I32, at=AT_X1)]
-        x_plane = sbuf("x_plane", [P, WINDOW], U8)
+        x_sb = sbuf("x_sb", [P, PASSES, WINDOW], I32)
+        x_plane = sbuf("x_plane", [P, PLANE_WINDOW], U8)
         wa_sb = [sbuf(f"wa_sb{pair}", [P, PAIR * PASSES, 2 * H], U8) for pair in range(F // PAIR)]
         wa_plane = sbuf("wa_plane", [P, F * PASSES, H], U8)
-        w_sb = [sbuf(f"w_sb{half}", [P, E // 2 * PASSES, N], I32) for half in range(2)]
+        w_sb = sbuf("w_sb", [P, E * PASSES, N], I32)
         w_plane = sbuf("w_plane", [P, E * PASSES, N], U8)
         wb_sb = sbuf("wb_sb", [P, F, 2 * N], U8)
         wb_plane = sbuf("wb_plane", [P, F, N], U8)
-        gate_rows = sbuf("gate_rows", [P, P], F32)
+        gate_rows = sbuf("gate_rows", [P, P], F32, at=AT_GATE_ROWS)
         gate2_sb = sbuf("gate2_sb", [P, F * D], F32)
         ident = sbuf("ident", [P, P], F32)
         a_planes = [sbuf(f"a_plane{s}", [P, F * D], U8) for s in range(PASSES)]
 
-        nc.vector.memset(x_plane[:].bitcast(I32), 0)
-        for s in range(PASSES):
-            nc.vector.memset(x_sb[s][:, T:WINDOW], 0)
+        nc.gpsimd.memset(x_plane[:].bitcast(I32), 0)
+        nc.vector.memset(x_sb[:, :, T:WINDOW], 0)
         nc.vector.memset(wa_plane[:].rearrange("p a i -> p (a i)").bitcast(I32), 0)
         nc.vector.memset(a_planes[1][:].bitcast(I32), 0)
-        nc.vector.memset(w_plane[:].rearrange("p a n -> p (a n)").bitcast(I32), 0)
-        nc.vector.memset(wb_plane[:].rearrange("p a n -> p (a n)").bitcast(I32), 0)
         nc.vector.memset(gate_rows[:], 0.0)
-        make_identity(nc, ident[:])
+        nc.vector.memset(w_plane[:].rearrange("p a n -> p (a n)").bitcast(I32), 0)
+        nc.gpsimd.memset(wb_plane[:].rearrange("p a n -> p (a n)").bitcast(I32), 0)
 
-        def load_plane(plane, scales):
+        def load_plane(plane, scales, queue):
             rows = scales.rearrange("m s (q j) c -> j q (m s) c", j=SCALE_ROWS)
             for j in range(SCALE_ROWS):
-                nc.sync.dma_start(out=plane[j:P:QUADRANT].bitcast(I32), in_=rows[j].bitcast(I32))
+                queue.dma_start(out=plane[j:P:QUADRANT].bitcast(I32), in_=rows[j].bitcast(I32))
 
-        x_view = x_words.rearrange("s p t d -> s p (t d)").bitcast(I32)
+        x_view = x_words.rearrange("s p t d -> p s (t d)").bitcast(I32)
         wa_view = wa_words.rearrange("f s p b -> p (f s) b").bitcast(I32)
         w_view = w_words.rearrange("e s p n d -> p (e s) (n d)").bitcast(I32)
         nc.sync.dma_start(offs2_sb[:], offs2)
-        nc.sync.dma_start(pos_sb[0][:], pos1)
         for q in range(P // QUADRANT):
-            nc.sync.dma_start(
+            (nc.sync, nc.scalar)[q % 2].dma_start(
                 out=x_plane[QUADRANT * q : QUADRANT * q + PASSES * SCALE_ROWS, 0:T].bitcast(I32),
                 in_=x_scales[:, SCALE_ROWS * q : SCALE_ROWS * (q + 1), :].bitcast(I32))
-        for s in range(PASSES):
-            nc.sync.dma_start(out=x_sb[s][:, 0:T], in_=x_view[s])
+        nc.sync.dma_start(out=x_sb[:, :, 0:T], in_=x_view)
         nc.sync.dma_start(out=wa_sb[0][:].bitcast(I32), in_=wa_view[:, 0 : PAIR * PASSES, :])
-        load_plane(wa_plane[:], wa_scales)
+        load_plane(wa_plane[:], wa_scales, nc.sync)
         nc.sync.dma_start(offs_sb[:], offs)
         nc.sync.dma_start(out=wa_sb[1][:].bitcast(I32), in_=wa_view[:, PAIR * PASSES : F * PASSES, :])
-        nc.sync.dma_start(out=wb_sb[:].bitcast(I32), in_=wb_words.rearrange("f s p b -> p (f s) b").bitcast(I32))
-        load_plane(wb_plane[:], wb_scales)
         nc.sync.dma_start(out=gate_rows[0 : CHOICES * TOKEN_BLOCKS, :],
                           in_=gate[:, 0, :].rearrange("r (c t) -> r c t", t=P))
-        nc.sync.dma_start(out=w_sb[0][:], in_=w_view[:, 0 : E // 2 * PASSES, :])
-        load_plane(w_plane[:], w_scales)
-        nc.sync.dma_start(out=w_sb[1][:], in_=w_view[:, E // 2 * PASSES : E * PASSES, :])
+        nc.sync.dma_start(out=w_sb[:], in_=w_view)
+        load_plane(w_plane[:], w_scales, nc.sync)
+        nc.sync.dma_start(out=wb_sb[:].bitcast(I32), in_=wb_words.rearrange("f s p b -> p (f s) b").bitcast(I32))
+        load_plane(wb_plane[:], wb_scales, nc.gpsimd)
         nc.sync.dma_start(out=gate2_sb[:], in_=gate2)
-        nc.sync.dma_start(pos_sb[1][:], pos2)
+        for r, pos in enumerate((pos1, pos2)):
+            nc.sync.dma_start(pos_sb[r][:], pos)
 
-        x_windows = [x_sb[s][:].bitcast(U32) for s in range(PASSES)]
+        make_identity(nc, ident[:])
+
+        x_windows = [x_sb[:, s, :].bitcast(U32) for s in range(PASSES)]
         a_words = [sbuf(f"a_words{s}", [P, F * D], U32) for s in range(PASSES)]
         nc.vector.tensor_copy(a_planes[0][:], x_plane[:].indirect(offs2_sb[:]))
         nc.scalar.dma_start(out=a_planes[1][0:MOVED_ROWS, :].bitcast(I32),
@@ -141,52 +134,68 @@ def tile_moe_mlr_silu_kernel(
                         rhs=wa_sb[pair][:, g * PASSES + s, :].bitcast(FP4X4), rhs_scale=wa_plane[:, f * PASSES + s, :],
                         start=(s == 0), stop=(s == PASSES - 1))
 
-        h_bf = [sbuf(f"h_bf{pair}", [P, 4 * PAIR_SLOTS], BF16, at=at) for pair, at in enumerate((AT_H0, AT_H1))]
-        h_rows = [sbuf(f"h_rows{f}", [P, H], BF16) for f in range(F)]
-        for pair in range(F // PAIR):
-            shape = [P, PAIR, 2, D]
-            turned = turn_bank("turned0", shape) if pair == 0 else own_bank("turned1", shape, "first")
-            for g in range(PAIR):
-                f = PAIR * pair + g
-                nc.scalar.activation(
-                    out=h_rows[f][:].rearrange("m (u p e) -> m u p e", u=2, e=2),
-                    in_=pre[f][:].rearrange("m (p u e) -> m u p e", u=2, e=2), func=ACT.Silu)
-                for u in range(2):
-                    nc.tensor.transpose(turned[:, g, u, :], h_rows[f][:].bitcast(F32)[:, u * P : (u + 1) * P], ident[:])
-            nc.scalar.copy(
-                out=h_bf[pair][:].bitcast(F32).rearrange("p (g m u) -> p g m u", g=PAIR, u=2),
-                in_=turned[:].rearrange("p g u m -> p g m u"))
+        h_bf = [sbuf(f"h_bf{pair}", [P, 4 * PAIR_SLOTS], BF16) for pair in range(F // PAIR)]
+        y_sb = sbuf("y_sb", [P, E * C], F32)
+        h_rows = [sbuf(f"h_rows{f}", [P, H], BF16)[:] for f in range(F - 1)] + [y_sb[:, (E - 2) * C : E * C].bitcast(BF16)]
 
-        gate_turned = turn_bank("gate_turned", [P, P])
+        def activate(f):
+            nc.scalar.activation(
+                out=h_rows[f].rearrange("m (u p e) -> m u p e", u=2, e=2),
+                in_=pre[f][:].rearrange("m (p u e) -> m u p e", u=2, e=2), func=ACT.Silu)
+
+        def turn(f, turned):
+            for u in range(2):
+                nc.tensor.transpose(turned[:, u * D : (u + 1) * D], h_rows[f].bitcast(F32)[:, u * P : (u + 1) * P], ident[:])
+
+        def lay_out(f, turned):
+            pair, g = divmod(f, PAIR)
+            nc.scalar.copy(
+                out=h_bf[pair][:].bitcast(F32).rearrange("p (g m u) -> p g m u", g=PAIR, u=2)[:, g],
+                in_=turned.rearrange("p (u m) -> p m u", u=2))
+
+        def turn_and_lay_out(f, tag):
+            turned = own_bank(f"turned{f}", [P, 2 * D], tag)[:]
+            turn(f, turned)
+            lay_out(f, turned)
+
+        activate(0)
+        activate(1)
+        turn_and_lay_out(0, "a")
+        turn_and_lay_out(1, "b")
+        activate(2)
+        activate(3)
+        turn_and_lay_out(2, "a")
+
+        gate_turned = own_bank("gate_turned", [P, P], "b")
         nc.tensor.transpose(gate_turned[:], gate_rows[:], ident[:])
         gate_cols = sbuf("gate_cols", [P, CHOICES * TOKEN_BLOCKS], F32)
         nc.scalar.copy(out=gate_cols[:], in_=gate_turned[:, 0 : CHOICES * TOKEN_BLOCKS])
-
-        y_sb = sbuf("y_sb", [P, E * C], F32)
 
         def gather_slots(name, window, first, count, dtype, at=None):
             gathered = sbuf(name, [P, count * C], dtype, at=at)
             nc.vector.tensor_copy(gathered[:], window.indirect(entries(offs_sb, first * C, count * C)))
             return gathered
 
-        def experts(first, count, words, plane, tag):
-            y_ps = own_bank(f"y_ps{first}", [P, count * C], tag)
+        def experts(first, count, words, plane, plane_first, y_ps):
             for g in range(count):
-                half, place = divmod(first + g, E // 2)
+                place = first + g - plane_first
                 slots = slice(g * C, (g + 1) * C)
                 for s in range(PASSES):
                     nc.tensor.matmul_mx(
                         out=y_ps[:, slots],
-                        lhsT=w_sb[half][:, place * PASSES + s, :].bitcast(FP8X4),
+                        lhsT=w_sb[:, (first + g) * PASSES + s, :].bitcast(FP8X4),
                         lhsT_scale=w_plane[:, (first + g) * PASSES + s, :],
                         rhs=words[s][:, slots].bitcast(FP8X4),
                         rhs_scale=plane[SCALE_ROWS * s : P, place * C : (place + 1) * C],
                         start=(s == 0), stop=(s == PASSES - 1))
-            nc.scalar.copy(out=y_sb[:, first * C : (first + count) * C], in_=y_ps[:])
 
-        def second_layer(pair, z_ps):
+        def keep_y(first, count, y_ps):
+            nc.scalar.copy(out=y_sb[:, first * C : (first + count) * C], in_=y_ps)
+
+        def second_layer(pair, tag):
             h_codes = sbuf(f"h_codes{pair}", [P, PAIR_SLOTS], U32)
             h_plane = sbuf(f"h_plane{pair}", [P, PAIR_SLOTS], U8)
+            z_ps = own_bank(f"z_ps{pair}", [P, PAIR_SLOTS], tag)
             nc.vector.quantize_mx(out=h_codes[:].bitcast(FP8X4), scales=h_plane[:], in_=h_bf[pair][:])
             for g in range(PAIR):
                 f = PAIR * pair + g
@@ -203,19 +212,27 @@ def tile_moe_mlr_silu_kernel(
             nc.vector.tensor_tensor(adapted[:].indirect(entries(offs2_sb, first, PAIR_SLOTS)),
                                     z_sb[:], gate2_sb[:, first : first + PAIR_SLOTS], ALU.mult)
 
+        plane0 = gather_slots("plane0", x_plane[:], 0, 6, U8)
         words = [gather_slots(f"words0_{s}", x_windows[s], 0, 4, U32) for s in range(PASSES)]
-        plane = gather_slots("plane0", x_plane[:], 0, E // 2, U8)
-        experts(0, 4, words, plane, "first")
-        plane = gather_slots("plane1", x_plane[:], E // 2, E // 2, U8)
-        words = [gather_slots(f"words4_{s}", x_windows[s], 4, 2, U32) for s in range(PASSES)]
-        experts(4, 2, words, plane, "first")
-        z_first = second_layer(0, ring_bank("z_ps0", [P, PAIR_SLOTS]))
-        words = [gather_slots(f"words6_{s}", x_windows[s], 6, 2, U32, at=AT_H0 + 4 * 2 * C * s) for s in range(PASSES)]
-        experts(6, 2, words, plane, "second")
-        z_second = second_layer(1, own_bank("z_ps1", [P, PAIR_SLOTS], "second"))
+        y_ps = own_bank("y_ps0", [P, 4 * C], "b")[:]
+        experts(0, 4, words, plane0, 0, y_ps)
+        keep_y(0, 4, y_ps)
+        words4 = [gather_slots(f"words4_{s}", x_windows[s], 4, 2, U32) for s in range(PASSES)]
+        y_ps = own_bank("y_ps4", [P, 2 * C], "a")[:]
+        experts(4, 2, words4, plane0, 0, y_ps)
+        keep_y(4, 2, y_ps)
+        plane6 = gather_slots("plane6", x_plane[:], 6, 2, U8)
+        z_first = second_layer(0, "b")
+        words = [gather_slots(f"words6_{s}", x_windows[s], 6, 2, U32, at=AT_WORDS6 + 4 * 2 * C * s) for s in range(PASSES)]
+        turn_and_lay_out(3, "b")
+        y_ps = own_bank("y_ps6", [P, 2 * C], "a")[:]
+        experts(6, 2, words, plane6, 6, y_ps)
+        keep_y(6, 2, y_ps)
 
-        adapted = sbuf("adapted", [P, T], F32, at=AT_ADAPTED)
+        adapted = sbuf("adapted", [P, T], F32)
         scatter(adapted, 0, z_first)
+        z_second = second_layer(1, "a")
+
 
         def gated_choice(r, first, count, at=None):
             picked = sbuf(f"picked{r}_{first}", [P, count * P], F32, at=at)
@@ -230,11 +247,11 @@ def tile_moe_mlr_silu_kernel(
                                      scale=gate_cols[:, column : column + 1])
             return [scaled[:, c, :] for c in range(count)]
 
-        gated = [gated_choice(0, 0, TOKEN_BLOCKS, at=AT_CHOICE0),
-                 gated_choice(1, 0, HALF_BLOCKS) + gated_choice(1, HALF_BLOCKS, HALF_BLOCKS)]
+        halves = [[gated_choice(r, first, HALF_BLOCKS) for r in range(CHOICES)] for first in (0, HALF_BLOCKS)]
+        gated = [halves[0][r] + halves[1][r] for r in range(CHOICES)]
         scatter(adapted, 1, z_second)
 
-        for half, tag in enumerate(("first", "second")):
+        for half, tag in enumerate(("c", "b")):
             o_ps = own_bank(f"o_ps{half}", [P, HALF_BLOCKS * P], tag)
             for c in range(HALF_BLOCKS):
                 for r in range(CHOICES):

@@ -31,8 +31,11 @@ PAIR_SLOTS = PAIR * D
 TOKEN_BLOCKS = T // P
 HALF_BLOCKS = TOKEN_BLOCKS // 2
 
-AT_WORDS6 = 0
-AT_GATE_ROWS = 768
+AT_WORDS4 = 0
+AT_PLANE6 = AT_WORDS4 + 4 * 2 * C
+AT_WORDS6 = AT_PLANE6 + 2 * C
+AT_GATE_ROWS = AT_PLANE6 - 128
+AT_X_PLANE = 4096
 
 
 def tile_moe_mlr_silu_kernel(
@@ -63,11 +66,11 @@ def tile_moe_mlr_silu_kernel(
         offs2_sb = keep.tile([P, F * D // LIST_ROWS], U16, name="offs2_sb")
         pos_sb = [keep.tile([P, T // LIST_ROWS], U16, name=f"pos_sb{r}") for r in range(CHOICES)]
 
-        x_sb = sbuf("x_sb", [P, PASSES, WINDOW], I32)
-        x_plane = sbuf("x_plane", [P, PLANE_WINDOW], U8)
+        x_sb = [sbuf(f"x_sb{s}", [P, WINDOW], I32) for s in range(PASSES)]
+        x_plane = sbuf("x_plane", [P, PLANE_WINDOW], U8, at=AT_X_PLANE)
         wa_sb = [sbuf(f"wa_sb{pair}", [P, PAIR * PASSES, 2 * H], U8) for pair in range(F // PAIR)]
         wa_plane = sbuf("wa_plane", [P, F * PASSES, H], U8)
-        w_sb = sbuf("w_sb", [P, E * PASSES, N], I32)
+        w_sb = [sbuf(f"w_sb{half}", [P, E // 2 * PASSES, N], I32) for half in range(2)]
         w_plane = sbuf("w_plane", [P, E * PASSES, N], U8)
         wb_sb = sbuf("wb_sb", [P, F, 2 * N], U8)
         wb_plane = sbuf("wb_plane", [P, F, N], U8)
@@ -76,45 +79,48 @@ def tile_moe_mlr_silu_kernel(
         ident = sbuf("ident", [P, P], F32)
         a_planes = [sbuf(f"a_plane{s}", [P, F * D], U8) for s in range(PASSES)]
 
-        nc.gpsimd.memset(x_plane[:].bitcast(I32), 0)
-        nc.vector.memset(x_sb[:, :, T:WINDOW], 0)
+        nc.vector.memset(x_plane[:].bitcast(I32), 0)
+        for s in range(PASSES):
+            nc.vector.memset(x_sb[s][:, T:WINDOW], 0)
         nc.vector.memset(wa_plane[:].rearrange("p a i -> p (a i)").bitcast(I32), 0)
         nc.vector.memset(a_planes[1][:].bitcast(I32), 0)
         nc.vector.memset(gate_rows[:], 0.0)
         nc.vector.memset(w_plane[:].rearrange("p a n -> p (a n)").bitcast(I32), 0)
-        nc.gpsimd.memset(wb_plane[:].rearrange("p a n -> p (a n)").bitcast(I32), 0)
+        nc.vector.memset(wb_plane[:].rearrange("p a n -> p (a n)").bitcast(I32), 0)
+        nc.vector.memset(ident[:], 0.0)
+        make_identity(nc, ident[:], nomemset=True)
 
-        def load_plane(plane, scales, queue):
+        def load_plane(plane, scales):
             rows = scales.rearrange("m s (q j) c -> j q (m s) c", j=SCALE_ROWS)
             for j in range(SCALE_ROWS):
-                queue.dma_start(out=plane[j:P:QUADRANT].bitcast(I32), in_=rows[j].bitcast(I32))
+                nc.sync.dma_start(out=plane[j:P:QUADRANT].bitcast(I32), in_=rows[j].bitcast(I32))
 
-        x_view = x_words.rearrange("s p t d -> p s (t d)").bitcast(I32)
+        x_view = x_words.rearrange("s p t d -> s p (t d)").bitcast(I32)
         wa_view = wa_words.rearrange("f s p b -> p (f s) b").bitcast(I32)
         w_view = w_words.rearrange("e s p n d -> p (e s) (n d)").bitcast(I32)
         nc.sync.dma_start(offs2_sb[:], offs2)
+        nc.sync.dma_start(pos_sb[0][:], pos1)
         for q in range(P // QUADRANT):
-            (nc.sync, nc.scalar)[q % 2].dma_start(
+            nc.sync.dma_start(
                 out=x_plane[QUADRANT * q : QUADRANT * q + PASSES * SCALE_ROWS, 0:T].bitcast(I32),
                 in_=x_scales[:, SCALE_ROWS * q : SCALE_ROWS * (q + 1), :].bitcast(I32))
-        nc.sync.dma_start(out=x_sb[:, :, 0:T], in_=x_view)
+        for s in range(PASSES):
+            nc.sync.dma_start(out=x_sb[s][:, 0:T], in_=x_view[s])
         nc.sync.dma_start(out=wa_sb[0][:].bitcast(I32), in_=wa_view[:, 0 : PAIR * PASSES, :])
-        load_plane(wa_plane[:], wa_scales, nc.sync)
+        load_plane(wa_plane[:], wa_scales)
         nc.sync.dma_start(offs_sb[:], offs)
         nc.sync.dma_start(out=wa_sb[1][:].bitcast(I32), in_=wa_view[:, PAIR * PASSES : F * PASSES, :])
         nc.sync.dma_start(out=gate_rows[0 : CHOICES * TOKEN_BLOCKS, :],
                           in_=gate[:, 0, :].rearrange("r (c t) -> r c t", t=P))
-        nc.sync.dma_start(out=w_sb[:], in_=w_view)
-        load_plane(w_plane[:], w_scales, nc.sync)
+        nc.sync.dma_start(out=w_sb[0][:], in_=w_view[:, 0 : E // 2 * PASSES, :])
+        load_plane(w_plane[:], w_scales)
         nc.sync.dma_start(out=wb_sb[:].bitcast(I32), in_=wb_words.rearrange("f s p b -> p (f s) b").bitcast(I32))
-        load_plane(wb_plane[:], wb_scales, nc.gpsimd)
+        load_plane(wb_plane[:], wb_scales)
+        nc.sync.dma_start(out=w_sb[1][:], in_=w_view[:, E // 2 * PASSES : E * PASSES, :])
         nc.sync.dma_start(out=gate2_sb[:], in_=gate2)
-        for r, pos in enumerate((pos1, pos2)):
-            nc.sync.dma_start(pos_sb[r][:], pos)
+        nc.sync.dma_start(pos_sb[1][:], pos2)
 
-        make_identity(nc, ident[:])
-
-        x_windows = [x_sb[:, s, :].bitcast(U32) for s in range(PASSES)]
+        x_windows = [x_sb[s][:].bitcast(U32) for s in range(PASSES)]
         a_words = [sbuf(f"a_words{s}", [P, F * D], U32) for s in range(PASSES)]
         nc.vector.tensor_copy(a_planes[0][:], x_plane[:].indirect(offs2_sb[:]))
         nc.scalar.dma_start(out=a_planes[1][0:MOVED_ROWS, :].bitcast(I32),
@@ -136,7 +142,7 @@ def tile_moe_mlr_silu_kernel(
 
         h_bf = [sbuf(f"h_bf{pair}", [P, 4 * PAIR_SLOTS], BF16) for pair in range(F // PAIR)]
         y_sb = sbuf("y_sb", [P, E * C], F32)
-        h_rows = [sbuf(f"h_rows{f}", [P, H], BF16)[:] for f in range(F - 1)] + [y_sb[:, (E - 2) * C : E * C].bitcast(BF16)]
+        h_rows = [sbuf(f"h_rows{f}", [P, H], BF16)[:] for f in range(F)]
 
         def activate(f):
             nc.scalar.activation(
@@ -164,17 +170,19 @@ def tile_moe_mlr_silu_kernel(
         turn_and_lay_out(1, "b")
         activate(2)
         activate(3)
-        turn_and_lay_out(2, "a")
+        turn_and_lay_out(2, "c")
 
         gate_turned = own_bank("gate_turned", [P, P], "b")
         nc.tensor.transpose(gate_turned[:], gate_rows[:], ident[:])
         gate_cols = sbuf("gate_cols", [P, CHOICES * TOKEN_BLOCKS], F32)
         nc.scalar.copy(out=gate_cols[:], in_=gate_turned[:, 0 : CHOICES * TOKEN_BLOCKS])
 
+        turn_and_lay_out(3, "b")
+
         def gather_slots(name, window, first, count, dtype, at=None):
             gathered = sbuf(name, [P, count * C], dtype, at=at)
             nc.vector.tensor_copy(gathered[:], window.indirect(entries(offs_sb, first * C, count * C)))
-            return gathered
+            return gathered[:]
 
         def experts(first, count, words, plane, plane_first, y_ps):
             for g in range(count):
@@ -183,7 +191,7 @@ def tile_moe_mlr_silu_kernel(
                 for s in range(PASSES):
                     nc.tensor.matmul_mx(
                         out=y_ps[:, slots],
-                        lhsT=w_sb[:, (first + g) * PASSES + s, :].bitcast(FP8X4),
+                        lhsT=w_sb[(first + g) // (E // 2)][:, (first + g) % (E // 2) * PASSES + s, :].bitcast(FP8X4),
                         lhsT_scale=w_plane[:, (first + g) * PASSES + s, :],
                         rhs=words[s][:, slots].bitcast(FP8X4),
                         rhs_scale=plane[SCALE_ROWS * s : P, place * C : (place + 1) * C],
@@ -214,22 +222,22 @@ def tile_moe_mlr_silu_kernel(
 
         plane0 = gather_slots("plane0", x_plane[:], 0, 6, U8)
         words = [gather_slots(f"words0_{s}", x_windows[s], 0, 4, U32) for s in range(PASSES)]
-        y_ps = own_bank("y_ps0", [P, 4 * C], "b")[:]
+        y_ps = own_bank("y_ps0", [P, 4 * C], "a")[:]
         experts(0, 4, words, plane0, 0, y_ps)
         keep_y(0, 4, y_ps)
-        words4 = [gather_slots(f"words4_{s}", x_windows[s], 4, 2, U32) for s in range(PASSES)]
-        y_ps = own_bank("y_ps4", [P, 2 * C], "a")[:]
-        experts(4, 2, words4, plane0, 0, y_ps)
+        late0 = gather_slots("words4_0", x_windows[0], 4, 4, U32)
+        z_first = second_layer(0, "d")
+        words4 = gather_slots("words4_1", x_windows[1], 4, 2, U32, at=AT_WORDS4)
+        y_ps = own_bank("y_ps4", [P, 2 * C], "c")[:]
+        experts(4, 2, [late0[:, 0 : 2 * C], words4], plane0, 0, y_ps)
         keep_y(4, 2, y_ps)
-        plane6 = gather_slots("plane6", x_plane[:], 6, 2, U8)
-        z_first = second_layer(0, "b")
-        words = [gather_slots(f"words6_{s}", x_windows[s], 6, 2, U32, at=AT_WORDS6 + 4 * 2 * C * s) for s in range(PASSES)]
-        turn_and_lay_out(3, "b")
+        plane6 = gather_slots("plane6", x_plane[:], 6, 2, U8, at=AT_PLANE6)
+        words6 = gather_slots("words6_1", x_windows[1], 6, 2, U32, at=AT_WORDS6)
         y_ps = own_bank("y_ps6", [P, 2 * C], "a")[:]
-        experts(6, 2, words, plane6, 6, y_ps)
+        experts(6, 2, [late0[:, 2 * C : 4 * C], words6], plane6, 6, y_ps)
         keep_y(6, 2, y_ps)
 
-        adapted = sbuf("adapted", [P, T], F32)
+        adapted = sbuf("adapted", [P, T], F32, at=AT_X_PLANE)
         scatter(adapted, 0, z_first)
         z_second = second_layer(1, "a")
 
@@ -251,7 +259,7 @@ def tile_moe_mlr_silu_kernel(
         gated = [halves[0][r] + halves[1][r] for r in range(CHOICES)]
         scatter(adapted, 1, z_second)
 
-        for half, tag in enumerate(("c", "b")):
+        for half, tag in enumerate(("c", "d")):
             o_ps = own_bank(f"o_ps{half}", [P, HALF_BLOCKS * P], tag)
             for c in range(HALF_BLOCKS):
                 for r in range(CHOICES):

@@ -90,10 +90,10 @@ def tile_moe_mlr_silu_kernel(
         nc.vector.memset(ident[:], 0.0)
         make_identity(nc, ident[:], nomemset=True)
 
-        def load_plane(plane, scales):
+        def load_plane(plane, scales, queue):
             rows = scales.rearrange("m s (q j) c -> j q (m s) c", j=SCALE_ROWS)
             for j in range(SCALE_ROWS):
-                nc.sync.dma_start(out=plane[j:P:QUADRANT].bitcast(I32), in_=rows[j].bitcast(I32))
+                queue.dma_start(out=plane[j:P:QUADRANT].bitcast(I32), in_=rows[j].bitcast(I32))
 
         x_view = x_words.rearrange("s p t d -> s p (t d)").bitcast(I32)
         wa_view = wa_words.rearrange("f s p b -> p (f s) b").bitcast(I32)
@@ -107,15 +107,15 @@ def tile_moe_mlr_silu_kernel(
         for s in range(PASSES):
             nc.sync.dma_start(out=x_sb[s][:, 0:T], in_=x_view[s])
         nc.sync.dma_start(out=wa_sb[0][:].bitcast(I32), in_=wa_view[:, 0 : PAIR * PASSES, :])
-        load_plane(wa_plane[:], wa_scales)
+        load_plane(wa_plane[:], wa_scales, nc.sync)
         nc.sync.dma_start(offs_sb[:], offs)
         nc.sync.dma_start(out=wa_sb[1][:].bitcast(I32), in_=wa_view[:, PAIR * PASSES : F * PASSES, :])
         nc.sync.dma_start(out=gate_rows[0 : CHOICES * TOKEN_BLOCKS, :],
                           in_=gate[:, 0, :].rearrange("r (c t) -> r c t", t=P))
         nc.sync.dma_start(out=w_sb[0][:], in_=w_view[:, 0 : E // 2 * PASSES, :])
-        load_plane(w_plane[:], w_scales)
+        load_plane(w_plane[:], w_scales, nc.sync)
         nc.sync.dma_start(out=wb_sb[:].bitcast(I32), in_=wb_words.rearrange("f s p b -> p (f s) b").bitcast(I32))
-        load_plane(wb_plane[:], wb_scales)
+        load_plane(wb_plane[:], wb_scales, nc.gpsimd)
         nc.sync.dma_start(out=w_sb[1][:], in_=w_view[:, E // 2 * PASSES : E * PASSES, :])
         nc.sync.dma_start(out=gate2_sb[:], in_=gate2)
         nc.sync.dma_start(pos_sb[1][:], pos2)
@@ -177,7 +177,7 @@ def tile_moe_mlr_silu_kernel(
         gate_cols = sbuf("gate_cols", [P, CHOICES * TOKEN_BLOCKS], F32)
         nc.scalar.copy(out=gate_cols[:], in_=gate_turned[:, 0 : CHOICES * TOKEN_BLOCKS])
 
-        turn_and_lay_out(3, "b")
+        turn_and_lay_out(3, "a")
 
         def gather_slots(name, window, first, count, dtype, at=None):
             gathered = sbuf(name, [P, count * C], dtype, at=at)
@@ -222,7 +222,7 @@ def tile_moe_mlr_silu_kernel(
 
         plane0 = gather_slots("plane0", x_plane[:], 0, 6, U8)
         words = [gather_slots(f"words0_{s}", x_windows[s], 0, 4, U32) for s in range(PASSES)]
-        y_ps = own_bank("y_ps0", [P, 4 * C], "a")[:]
+        y_ps = own_bank("y_ps0", [P, 4 * C], "b")[:]
         experts(0, 4, words, plane0, 0, y_ps)
         keep_y(0, 4, y_ps)
         late0 = gather_slots("words4_0", x_windows[0], 4, 4, U32)

@@ -79,16 +79,15 @@ def tile_moe_mlr_silu_kernel(
         ident = sbuf("ident", [P, P], F32)
         a_planes = [sbuf(f"a_plane{s}", [P, F * D], U8) for s in range(PASSES)]
 
-        nc.vector.memset(x_plane[:].bitcast(I32), 0)
+        nc.gpsimd.memset(x_plane[:].bitcast(I32), 0)
         for s in range(PASSES):
             nc.vector.memset(x_sb[s][:, T:WINDOW], 0)
         nc.vector.memset(wa_plane[:].rearrange("p a i -> p (a i)").bitcast(I32), 0)
         nc.vector.memset(a_planes[1][:].bitcast(I32), 0)
         nc.vector.memset(gate_rows[:], 0.0)
         nc.vector.memset(w_plane[:].rearrange("p a n -> p (a n)").bitcast(I32), 0)
-        nc.vector.memset(wb_plane[:].rearrange("p a n -> p (a n)").bitcast(I32), 0)
-        nc.vector.memset(ident[:], 0.0)
-        make_identity(nc, ident[:], nomemset=True)
+        nc.gpsimd.memset(wb_plane[:].rearrange("p a n -> p (a n)").bitcast(I32), 0)
+        make_identity(nc, ident[:])
 
         def load_plane(plane, scales, queue):
             rows = scales.rearrange("m s (q j) c -> j q (m s) c", j=SCALE_ROWS)
@@ -99,9 +98,8 @@ def tile_moe_mlr_silu_kernel(
         wa_view = wa_words.rearrange("f s p b -> p (f s) b").bitcast(I32)
         w_view = w_words.rearrange("e s p n d -> p (e s) (n d)").bitcast(I32)
         nc.sync.dma_start(offs2_sb[:], offs2)
-        nc.sync.dma_start(pos_sb[0][:], pos1)
         for q in range(P // QUADRANT):
-            nc.sync.dma_start(
+            (nc.sync, nc.scalar)[q % 2].dma_start(
                 out=x_plane[QUADRANT * q : QUADRANT * q + PASSES * SCALE_ROWS, 0:T].bitcast(I32),
                 in_=x_scales[:, SCALE_ROWS * q : SCALE_ROWS * (q + 1), :].bitcast(I32))
         for s in range(PASSES):
@@ -118,7 +116,8 @@ def tile_moe_mlr_silu_kernel(
         load_plane(wb_plane[:], wb_scales, nc.gpsimd)
         nc.sync.dma_start(out=w_sb[1][:], in_=w_view[:, E // 2 * PASSES : E * PASSES, :])
         nc.sync.dma_start(out=gate2_sb[:], in_=gate2)
-        nc.sync.dma_start(pos_sb[1][:], pos2)
+        for r, pos in enumerate((pos1, pos2)):
+            nc.sync.dma_start(pos_sb[r][:], pos)
 
         x_windows = [x_sb[s][:].bitcast(U32) for s in range(PASSES)]
         a_words = [sbuf(f"a_words{s}", [P, F * D], U32) for s in range(PASSES)]

@@ -26,15 +26,23 @@ SCALE_ROWS = 4
 MOVED_ROWS = 112
 WINDOW = 688
 PLANE_WINDOW = 1024
+FIRST_SCATTER = 224
+SCATTER_WINDOW = 2 * (F * D - FIRST_SCATTER)
 PAIR = 2
 PAIR_SLOTS = PAIR * D
 TOKEN_BLOCKS = T // P
 HALF_BLOCKS = TOKEN_BLOCKS // 2
 
-AT_WORDS4 = 0
-AT_PLANE6 = AT_WORDS4 + 4 * 2 * C
-AT_WORDS6 = AT_PLANE6 + 2 * C
-AT_GATE_ROWS = AT_PLANE6 - 128
+EARLY = 4
+LATE = 2
+MIDDLE_FIRST = EARLY
+LAST_FIRST = EARLY + LATE
+WORD_BYTES = 4
+
+AT_MIDDLE_WORDS = 0
+AT_LAST_PLANE = AT_MIDDLE_WORDS + WORD_BYTES * LATE * C
+AT_LAST_WORDS = AT_LAST_PLANE + LATE * C
+AT_GATE_ROWS = AT_LAST_PLANE - (WORD_BYTES * P - LATE * C) // 2
 AT_X_PLANE = 4096
 
 
@@ -141,63 +149,59 @@ def tile_moe_mlr_silu_kernel(
 
         h_bf = [sbuf(f"h_bf{pair}", [P, 4 * PAIR_SLOTS], BF16) for pair in range(F // PAIR)]
         y_sb = sbuf("y_sb", [P, E * C], F32)
-        h_rows = [sbuf(f"h_rows{f}", [P, H], BF16)[:] for f in range(F)]
+        h_rows = [sbuf(f"h_rows{f}", [P, H], BF16) for f in range(F)]
 
         def activate(f):
             nc.scalar.activation(
-                out=h_rows[f].rearrange("m (u p e) -> m u p e", u=2, e=2),
+                out=h_rows[f][:].rearrange("m (u p e) -> m u p e", u=2, e=2),
                 in_=pre[f][:].rearrange("m (p u e) -> m u p e", u=2, e=2), func=ACT.Silu)
 
-        def turn(f, turned):
+        def turn(f, tag):
+            turned = own_bank(f"turned{f}", [P, 2 * D], tag)
             for u in range(2):
-                nc.tensor.transpose(turned[:, u * D : (u + 1) * D], h_rows[f].bitcast(F32)[:, u * P : (u + 1) * P], ident[:])
-
-        def lay_out(f, turned):
+                nc.tensor.transpose(turned[:, u * D : (u + 1) * D],
+                                    h_rows[f][:].bitcast(F32)[:, u * P : (u + 1) * P], ident[:])
             pair, g = divmod(f, PAIR)
             nc.scalar.copy(
                 out=h_bf[pair][:].bitcast(F32).rearrange("p (g m u) -> p g m u", g=PAIR, u=2)[:, g],
-                in_=turned.rearrange("p (u m) -> p m u", u=2))
-
-        def turn_and_lay_out(f, tag):
-            turned = own_bank(f"turned{f}", [P, 2 * D], tag)[:]
-            turn(f, turned)
-            lay_out(f, turned)
+                in_=turned[:].rearrange("p (u m) -> p m u", u=2))
 
         activate(0)
         activate(1)
-        turn_and_lay_out(0, "a")
-        turn_and_lay_out(1, "b")
+        turn(0, "a")
+        turn(1, "b")
         activate(2)
         activate(3)
-        turn_and_lay_out(2, "c")
+        turn(2, "c")
 
         gate_turned = own_bank("gate_turned", [P, P], "b")
         nc.tensor.transpose(gate_turned[:], gate_rows[:], ident[:])
         gate_cols = sbuf("gate_cols", [P, CHOICES * TOKEN_BLOCKS], F32)
         nc.scalar.copy(out=gate_cols[:], in_=gate_turned[:, 0 : CHOICES * TOKEN_BLOCKS])
 
-        turn_and_lay_out(3, "a")
+        turn(3, "a")
 
         def gather_slots(name, window, first, count, dtype, at=None):
             gathered = sbuf(name, [P, count * C], dtype, at=at)
             nc.vector.tensor_copy(gathered[:], window.indirect(entries(offs_sb, first * C, count * C)))
             return gathered[:]
 
-        def experts(first, count, words, plane, plane_first, y_ps):
+        def experts(first, count, words, plane, tag):
+            y_ps = own_bank(f"y_ps{first}", [P, count * C], tag)
             for g in range(count):
-                place = first + g - plane_first
+                half, place = divmod(first + g, E // 2)
                 slots = slice(g * C, (g + 1) * C)
                 for s in range(PASSES):
                     nc.tensor.matmul_mx(
                         out=y_ps[:, slots],
-                        lhsT=w_sb[(first + g) // (E // 2)][:, (first + g) % (E // 2) * PASSES + s, :].bitcast(FP8X4),
+                        lhsT=w_sb[half][:, place * PASSES + s, :].bitcast(FP8X4),
                         lhsT_scale=w_plane[:, (first + g) * PASSES + s, :],
                         rhs=words[s][:, slots].bitcast(FP8X4),
-                        rhs_scale=plane[SCALE_ROWS * s : P, place * C : (place + 1) * C],
+                        rhs_scale=plane[SCALE_ROWS * s : P, slots],
                         start=(s == 0), stop=(s == PASSES - 1))
+            nc.scalar.copy(out=y_sb[:, first * C : (first + count) * C], in_=y_ps[:])
 
-        def keep_y(first, count, y_ps):
-            nc.scalar.copy(out=y_sb[:, first * C : (first + count) * C], in_=y_ps)
+        z_sb = sbuf("z_sb", [P, F * D], F32)
 
         def second_layer(pair, tag):
             h_codes = sbuf(f"h_codes{pair}", [P, PAIR_SLOTS], U32)
@@ -210,39 +214,30 @@ def tile_moe_mlr_silu_kernel(
                 nc.tensor.matmul_mx(
                     out=z_ps[:, slots], lhsT=wb_sb[:, f, :].bitcast(FP4X4), lhsT_scale=wb_plane[:, f, :],
                     rhs=h_codes[:, slots].bitcast(FP8X4), rhs_scale=h_plane[:, slots], start=True, stop=True)
-            z_sb = sbuf(f"z_sb{pair}", [P, PAIR_SLOTS], F32)
-            nc.scalar.copy(out=z_sb[:], in_=z_ps[:])
-            return z_sb
+            nc.scalar.copy(out=z_sb[:, pair * PAIR_SLOTS : (pair + 1) * PAIR_SLOTS], in_=z_ps[:])
 
-        def scatter(adapted, pair, z_sb):
-            first = pair * PAIR_SLOTS
-            nc.vector.tensor_tensor(adapted[:].indirect(entries(offs2_sb, first, PAIR_SLOTS)),
-                                    z_sb[:], gate2_sb[:, first : first + PAIR_SLOTS], ALU.mult)
+        def scatter(adapted, first, count):
+            nc.vector.tensor_tensor(adapted[:].indirect(entries(offs2_sb, first, count)),
+                                    z_sb[:, first : first + count], gate2_sb[:, first : first + count], ALU.mult)
 
-        plane0 = gather_slots("plane0", x_plane[:], 0, 6, U8)
-        words = [gather_slots(f"words0_{s}", x_windows[s], 0, 4, U32) for s in range(PASSES)]
-        y_ps = own_bank("y_ps0", [P, 4 * C], "b")[:]
-        experts(0, 4, words, plane0, 0, y_ps)
-        keep_y(0, 4, y_ps)
-        late0 = gather_slots("words4_0", x_windows[0], 4, 4, U32)
-        z_first = second_layer(0, "d")
-        words4 = gather_slots("words4_1", x_windows[1], 4, 2, U32, at=AT_WORDS4)
-        y_ps = own_bank("y_ps4", [P, 2 * C], "c")[:]
-        experts(4, 2, [late0[:, 0 : 2 * C], words4], plane0, 0, y_ps)
-        keep_y(4, 2, y_ps)
-        plane6 = gather_slots("plane6", x_plane[:], 6, 2, U8, at=AT_PLANE6)
-        words6 = gather_slots("words6_1", x_windows[1], 6, 2, U32, at=AT_WORDS6)
-        y_ps = own_bank("y_ps6", [P, 2 * C], "a")[:]
-        experts(6, 2, [late0[:, 2 * C : 4 * C], words6], plane6, 6, y_ps)
-        keep_y(6, 2, y_ps)
+        plane = gather_slots("plane", x_plane[:], 0, EARLY + LATE, U8)
+        early_words = [gather_slots(f"early_words{s}", x_windows[s], 0, EARLY, U32) for s in range(PASSES)]
+        experts(0, EARLY, early_words, plane[:, 0 : EARLY * C], "b")
+        late_words0 = gather_slots("late_words0", x_windows[0], MIDDLE_FIRST, 2 * LATE, U32)
+        second_layer(0, "d")
+        middle_words1 = gather_slots("middle_words1", x_windows[1], MIDDLE_FIRST, LATE, U32, at=AT_MIDDLE_WORDS)
+        experts(MIDDLE_FIRST, LATE, [late_words0[:, 0 : LATE * C], middle_words1],
+                plane[:, EARLY * C : (EARLY + LATE) * C], "c")
+        last_plane = gather_slots("last_plane", x_plane[:], LAST_FIRST, LATE, U8, at=AT_LAST_PLANE)
+        last_words1 = gather_slots("last_words1", x_windows[1], LAST_FIRST, LATE, U32, at=AT_LAST_WORDS)
+        experts(LAST_FIRST, LATE, [late_words0[:, LATE * C : 2 * LATE * C], last_words1], last_plane, "a")
 
-        adapted = sbuf("adapted", [P, T], F32, at=AT_X_PLANE)
-        scatter(adapted, 0, z_first)
-        z_second = second_layer(1, "a")
+        adapted = sbuf("adapted", [P, SCATTER_WINDOW], F32, at=AT_X_PLANE)
+        scatter(adapted, 0, FIRST_SCATTER)
+        second_layer(1, "a")
 
-
-        def gated_choice(r, first, count, at=None):
-            picked = sbuf(f"picked{r}_{first}", [P, count * P], F32, at=at)
+        def gated_choice(r, first, count):
+            picked = sbuf(f"picked{r}_{first}", [P, count * P], F32)
             nc.vector.tensor_copy(picked[:], y_sb[:].indirect(entries(pos_sb[r], first * P, count * P)))
             by_token = ring_bank(f"by_token{r}_{first}", [P, count, N])
             scaled = sbuf(f"scaled{r}_{first}", [P, count, N], F32)
@@ -256,7 +251,7 @@ def tile_moe_mlr_silu_kernel(
 
         halves = [[gated_choice(r, first, HALF_BLOCKS) for r in range(CHOICES)] for first in (0, HALF_BLOCKS)]
         gated = [halves[0][r] + halves[1][r] for r in range(CHOICES)]
-        scatter(adapted, 1, z_second)
+        scatter(adapted, FIRST_SCATTER, F * D - FIRST_SCATTER)
 
         for half, tag in enumerate(("c", "d")):
             o_ps = own_bank(f"o_ps{half}", [P, HALF_BLOCKS * P], tag)

@@ -74,7 +74,8 @@ def tile_moe_mlr_silu_kernel(
         offs2_sb = keep.tile([P, F * D // LIST_ROWS], U16, name="offs2_sb")
         pos_sb = [keep.tile([P, T // LIST_ROWS], U16, name=f"pos_sb{r}") for r in range(CHOICES)]
 
-        x_sb = [sbuf(f"x_sb{s}", [P, WINDOW], I32) for s in range(PASSES)]
+        x_sb = sbuf("x_sb", [P, T + WINDOW], I32)
+        x_first = [(PASSES - 1 - s) * T for s in range(PASSES)]
         x_plane = sbuf("x_plane", [P, PLANE_WINDOW], U8, at=AT_X_PLANE)
         wa_sb = [sbuf(f"wa_sb{pair}", [P, PAIR * PASSES, 2 * H], U8) for pair in range(F // PAIR)]
         wa_plane = sbuf("wa_plane", [P, F * PASSES, H], U8)
@@ -87,15 +88,16 @@ def tile_moe_mlr_silu_kernel(
         ident = sbuf("ident", [P, P], F32)
         a_planes = [sbuf(f"a_plane{s}", [P, F * D], U8) for s in range(PASSES)]
 
-        nc.gpsimd.memset(x_plane[:].bitcast(I32), 0)
-        for s in range(PASSES):
-            nc.vector.memset(x_sb[s][:, T:WINDOW], 0)
+        nc.vector.memset(x_plane[:, 0:T].bitcast(I32), 0)
         nc.vector.memset(wa_plane[:].rearrange("p a i -> p (a i)").bitcast(I32), 0)
+        nc.vector.memset(x_plane[:, T:PLANE_WINDOW].bitcast(I32), 0)
+        nc.vector.memset(x_sb[:, PASSES * T : T + WINDOW], 0)
         nc.vector.memset(a_planes[1][:].bitcast(I32), 0)
         nc.vector.memset(gate_rows[:], 0.0)
         nc.vector.memset(w_plane[:].rearrange("p a n -> p (a n)").bitcast(I32), 0)
-        nc.gpsimd.memset(wb_plane[:].rearrange("p a n -> p (a n)").bitcast(I32), 0)
-        make_identity(nc, ident[:])
+        nc.vector.memset(wb_plane[:].rearrange("p a n -> p (a n)").bitcast(I32), 0)
+        nc.vector.memset(ident[:], 0.0)
+        make_identity(nc, ident[:], nomemset=True)
 
         def load_plane(plane, scales, queue):
             rows = scales.rearrange("m s (q j) c -> j q (m s) c", j=SCALE_ROWS)
@@ -111,7 +113,7 @@ def tile_moe_mlr_silu_kernel(
                 out=x_plane[QUADRANT * q : QUADRANT * q + PASSES * SCALE_ROWS, 0:T].bitcast(I32),
                 in_=x_scales[:, SCALE_ROWS * q : SCALE_ROWS * (q + 1), :].bitcast(I32))
         for s in range(PASSES):
-            nc.sync.dma_start(out=x_sb[s][:, 0:T], in_=x_view[s])
+            nc.sync.dma_start(out=x_sb[:, x_first[s] : x_first[s] + T], in_=x_view[s])
         nc.sync.dma_start(out=wa_sb[0][:].bitcast(I32), in_=wa_view[:, 0 : PAIR * PASSES, :])
         load_plane(wa_plane[:], wa_scales, nc.sync)
         nc.sync.dma_start(offs_sb[:], offs)
@@ -121,13 +123,13 @@ def tile_moe_mlr_silu_kernel(
         nc.sync.dma_start(out=w_sb[0][:], in_=w_view[:, 0 : E // 2 * PASSES, :])
         load_plane(w_plane[:], w_scales, nc.sync)
         nc.sync.dma_start(out=wb_sb[:].bitcast(I32), in_=wb_words.rearrange("f s p b -> p (f s) b").bitcast(I32))
-        load_plane(wb_plane[:], wb_scales, nc.gpsimd)
+        load_plane(wb_plane[:], wb_scales, nc.sync)
         nc.sync.dma_start(out=w_sb[1][:], in_=w_view[:, E // 2 * PASSES : E * PASSES, :])
         nc.sync.dma_start(out=gate2_sb[:], in_=gate2)
         for r, pos in enumerate((pos1, pos2)):
             nc.sync.dma_start(pos_sb[r][:], pos)
 
-        x_windows = [x_sb[s][:].bitcast(U32) for s in range(PASSES)]
+        x_windows = [x_sb[:, x_first[s] : x_first[s] + WINDOW].bitcast(U32) for s in range(PASSES)]
         a_words = [sbuf(f"a_words{s}", [P, F * D], U32) for s in range(PASSES)]
         nc.vector.tensor_copy(a_planes[0][:], x_plane[:].indirect(offs2_sb[:]))
         nc.scalar.dma_start(out=a_planes[1][0:MOVED_ROWS, :].bitcast(I32),

@@ -1,7 +1,6 @@
 from contextlib import ExitStack
 
 import concourse.mybir as mybir
-from concourse.masks import make_identity
 
 K, T, E, C, F, D, H, N = 1024, 512, 8, 128, 4, 128, 512, 128
 FLOPS = 2 * K * N * E * C + 2 * K * H * F * D + 2 * H * N * F * D
@@ -34,16 +33,17 @@ TOKEN_BLOCKS = T // P
 HALF_BLOCKS = TOKEN_BLOCKS // 2
 
 EARLY = 4
-LATE = 2
-MIDDLE_FIRST = EARLY
-LAST_FIRST = EARLY + LATE
+MIDDLE = 3
+LAST = E - EARLY - MIDDLE
+LATE_PLANE = 2
 WORD_BYTES = 4
 
 AT_MIDDLE_WORDS = 0
-AT_LAST_PLANE = AT_MIDDLE_WORDS + WORD_BYTES * LATE * C
-AT_LAST_WORDS = AT_LAST_PLANE + LATE * C
-AT_GATE_ROWS = AT_LAST_PLANE - (WORD_BYTES * P - LATE * C) // 2
+AT_LAST_PLANE = AT_MIDDLE_WORDS + WORD_BYTES * MIDDLE * C
+AT_LAST_WORDS = AT_LAST_PLANE + LATE_PLANE * C
+AT_GATE_ROWS = AT_LAST_PLANE - (WORD_BYTES * P - LATE_PLANE * C) // 2
 AT_X_PLANE = 4096
+AT_Y = 8192
 
 
 def tile_moe_mlr_silu_kernel(
@@ -88,16 +88,17 @@ def tile_moe_mlr_silu_kernel(
         ident = sbuf("ident", [P, P], F32)
         a_planes = [sbuf(f"a_plane{s}", [P, F * D], U8) for s in range(PASSES)]
 
-        nc.vector.memset(x_plane[:, 0:T].bitcast(I32), 0)
+        column_less_row = sbuf("column_less_row", [P, P], I32)
+        nc.gpsimd.iota(column_less_row[:], [[1, P]], base=0, channel_multiplier=-1)
+        nc.vector.memset(x_plane[:, 0 : T + WORD_BYTES].bitcast(I32), 0)
         nc.vector.memset(wa_plane[:].rearrange("p a i -> p (a i)").bitcast(I32), 0)
-        nc.vector.memset(x_plane[:, T:PLANE_WINDOW].bitcast(I32), 0)
+        nc.vector.memset(x_plane[:, T + WORD_BYTES : PLANE_WINDOW].bitcast(I32), 0)
         nc.vector.memset(x_sb[:, PASSES * T : T + WINDOW], 0)
         nc.vector.memset(a_planes[1][:].bitcast(I32), 0)
         nc.vector.memset(gate_rows[:], 0.0)
         nc.vector.memset(w_plane[:].rearrange("p a n -> p (a n)").bitcast(I32), 0)
         nc.vector.memset(wb_plane[:].rearrange("p a n -> p (a n)").bitcast(I32), 0)
-        nc.vector.memset(ident[:], 0.0)
-        make_identity(nc, ident[:], nomemset=True)
+        nc.vector.tensor_scalar(ident[:], column_less_row[:], 0.0, None, ALU.is_equal)
 
         def load_plane(plane, scales, queue):
             rows = scales.rearrange("m s (q j) c -> j q (m s) c", j=SCALE_ROWS)
@@ -150,7 +151,7 @@ def tile_moe_mlr_silu_kernel(
                         start=(s == 0), stop=(s == PASSES - 1))
 
         h_bf = [sbuf(f"h_bf{pair}", [P, 4 * PAIR_SLOTS], BF16) for pair in range(F // PAIR)]
-        y_sb = sbuf("y_sb", [P, E * C], F32)
+        y_sb = sbuf("y_sb", [P, E * C], F32, at=AT_Y)
         h_rows = [sbuf(f"h_rows{f}", [P, H], BF16) for f in range(F)]
 
         def activate(f):
@@ -188,7 +189,7 @@ def tile_moe_mlr_silu_kernel(
             nc.vector.tensor_copy(gathered[:], window.indirect(entries(offs_sb, first * C, count * C)))
             return gathered[:]
 
-        def experts(first, count, words, plane, tag):
+        def experts(first, count, words, planes, tag):
             y_ps = own_bank(f"y_ps{first}", [P, count * C], tag)
             for g in range(count):
                 half, place = divmod(first + g, E // 2)
@@ -199,14 +200,14 @@ def tile_moe_mlr_silu_kernel(
                         lhsT=w_sb[half][:, place * PASSES + s, :].bitcast(FP8X4),
                         lhsT_scale=w_plane[:, (first + g) * PASSES + s, :],
                         rhs=words[s][:, slots].bitcast(FP8X4),
-                        rhs_scale=plane[SCALE_ROWS * s : P, slots],
+                        rhs_scale=planes[first + g][SCALE_ROWS * s : P, :],
                         start=(s == 0), stop=(s == PASSES - 1))
-            nc.scalar.copy(out=y_sb[:, first * C : (first + count) * C], in_=y_ps[:])
+            return lambda: nc.scalar.copy(out=y_sb[:, first * C : (first + count) * C], in_=y_ps[:])
 
         z_sb = sbuf("z_sb", [P, F * D], F32)
 
         def second_layer(pair, tag):
-            h_codes = sbuf(f"h_codes{pair}", [P, PAIR_SLOTS], U32)
+            h_codes = sbuf(f"h_codes{pair}", [P, PAIR_SLOTS], U32, at=AT_Y if pair == 0 else None)
             h_plane = sbuf(f"h_plane{pair}", [P, PAIR_SLOTS], U8)
             z_ps = own_bank(f"z_ps{pair}", [P, PAIR_SLOTS], tag)
             nc.vector.quantize_mx(out=h_codes[:].bitcast(FP8X4), scales=h_plane[:], in_=h_bf[pair][:])
@@ -222,17 +223,19 @@ def tile_moe_mlr_silu_kernel(
             nc.vector.tensor_tensor(adapted[:].indirect(entries(offs2_sb, first, count)),
                                     z_sb[:, first : first + count], gate2_sb[:, first : first + count], ALU.mult)
 
-        plane = gather_slots("plane", x_plane[:], 0, EARLY + LATE, U8)
+        plane = gather_slots("plane", x_plane[:], 0, E - LATE_PLANE, U8)
+        planes = [plane[:, e * C : (e + 1) * C] for e in range(E - LATE_PLANE)]
         early_words = [gather_slots(f"early_words{s}", x_windows[s], 0, EARLY, U32) for s in range(PASSES)]
-        experts(0, EARLY, early_words, plane[:, 0 : EARLY * C], "b")
-        late_words0 = gather_slots("late_words0", x_windows[0], MIDDLE_FIRST, 2 * LATE, U32)
+        early_copy = experts(0, EARLY, early_words, planes, "b")
+        late_words0 = gather_slots("late_words0", x_windows[0], EARLY, E - EARLY, U32)
         second_layer(0, "d")
-        middle_words1 = gather_slots("middle_words1", x_windows[1], MIDDLE_FIRST, LATE, U32, at=AT_MIDDLE_WORDS)
-        experts(MIDDLE_FIRST, LATE, [late_words0[:, 0 : LATE * C], middle_words1],
-                plane[:, EARLY * C : (EARLY + LATE) * C], "c")
-        last_plane = gather_slots("last_plane", x_plane[:], LAST_FIRST, LATE, U8, at=AT_LAST_PLANE)
-        last_words1 = gather_slots("last_words1", x_windows[1], LAST_FIRST, LATE, U32, at=AT_LAST_WORDS)
-        experts(LAST_FIRST, LATE, [late_words0[:, LATE * C : 2 * LATE * C], last_words1], last_plane, "a")
+        early_copy()
+        last_plane = gather_slots("last_plane", x_plane[:], E - LATE_PLANE, LATE_PLANE, U8, at=AT_LAST_PLANE)
+        planes.extend(last_plane[:, e * C : (e + 1) * C] for e in range(LATE_PLANE))
+        middle_words1 = gather_slots("middle_words1", x_windows[1], EARLY, MIDDLE, U32, at=AT_MIDDLE_WORDS)
+        experts(EARLY, MIDDLE, [late_words0[:, 0 : MIDDLE * C], middle_words1], planes, "c")()
+        last_words1 = gather_slots("last_words1", x_windows[1], EARLY + MIDDLE, LAST, U32, at=AT_LAST_WORDS)
+        experts(EARLY + MIDDLE, LAST, [late_words0[:, MIDDLE * C : (E - EARLY) * C], last_words1], planes, "a")()
 
         adapted = sbuf("adapted", [P, SCATTER_WINDOW], F32, at=AT_X_PLANE)
         scatter(adapted, 0, FIRST_SCATTER)
@@ -257,10 +260,11 @@ def tile_moe_mlr_silu_kernel(
 
         for half, tag in enumerate(("c", "d")):
             o_ps = own_bank(f"o_ps{half}", [P, HALF_BLOCKS * P], tag)
-            for c in range(HALF_BLOCKS):
-                for r in range(CHOICES):
+            for r in range(CHOICES):
+                for c in range(HALF_BLOCKS):
                     nc.tensor.matmul(o_ps[:, c * P : (c + 1) * P], gated[r][HALF_BLOCKS * half + c], ident[:],
-                                     is_transpose=True, start=(r == 0), stop=(r == CHOICES - 1))
+                                     is_transpose=True, start=(r == 0 and c == 0),
+                                     stop=(r == CHOICES - 1 and c == HALF_BLOCKS - 1))
             tokens = slice(half * HALF_BLOCKS * P, (half + 1) * HALF_BLOCKS * P)
             result = sbuf(f"result{half}", [P, HALF_BLOCKS * P], F32)
             nc.vector.tensor_tensor(result[:], o_ps[:], adapted[:, tokens], ALU.add)

@@ -24,8 +24,8 @@ QUADRANT = 32
 SCALE_ROWS = 4
 MOVED_ROWS = 112
 WINDOW = 688
-PLANE_WINDOW = 1024
-FIRST_SCATTER = 224
+PLANE_WINDOW = 1024 + 192
+FIRST_SCATTER = 256
 SCATTER_WINDOW = 2 * (F * D - FIRST_SCATTER)
 PAIR = 2
 PAIR_SLOTS = PAIR * D
@@ -35,7 +35,7 @@ HALF_BLOCKS = TOKEN_BLOCKS // 2
 EARLY = 4
 MIDDLE = 3
 LAST = E - EARLY - MIDDLE
-LATE_PLANE = 2
+LATE_PLANE = 1
 WORD_BYTES = 4
 
 AT_MIDDLE_WORDS = 0
@@ -60,9 +60,6 @@ def tile_moe_mlr_silu_kernel(
             if at is None:
                 return keep.tile(shape, dtype, name=name, align_bytes=64)
             return shared.tile(shape, dtype, name=name, offset=at, align_bytes=64)
-
-        def ring_bank(name, shape):
-            return psum.tile(shape, F32, name=name, tag="ring", bufs=4)
 
         def own_bank(name, shape, tag):
             return psum.tile(shape, F32, name=name, tag=tag)
@@ -138,7 +135,7 @@ def tile_moe_mlr_silu_kernel(
         for s in range(PASSES):
             nc.vector.tensor_copy(a_words[s][:], x_windows[s].indirect(offs2_sb[:]))
 
-        pre = [ring_bank(f"pre{f}", [P, H]) for f in range(F)]
+        pre = [own_bank(f"pre{f}", [P, H], f"first{f}") for f in range(F)]
         for pair in range(F // PAIR):
             for s in range(PASSES):
                 for g in range(PAIR):
@@ -230,7 +227,7 @@ def tile_moe_mlr_silu_kernel(
         late_words0 = gather_slots("late_words0", x_windows[0], EARLY, E - EARLY, U32)
         second_layer(0, "d")
         early_copy()
-        last_plane = gather_slots("last_plane", x_plane[:], E - LATE_PLANE, LATE_PLANE, U8, at=AT_LAST_PLANE)
+        last_plane = gather_slots("last_plane", x_plane[:, 0:T], E - LATE_PLANE, LATE_PLANE, U8, at=AT_LAST_PLANE)
         planes.extend(last_plane[:, e * C : (e + 1) * C] for e in range(LATE_PLANE))
         middle_words1 = gather_slots("middle_words1", x_windows[1], EARLY, MIDDLE, U32, at=AT_MIDDLE_WORDS)
         experts(EARLY, MIDDLE, [late_words0[:, 0 : MIDDLE * C], middle_words1], planes, "c")()
@@ -244,7 +241,7 @@ def tile_moe_mlr_silu_kernel(
         def gated_choice(r, first, count):
             picked = sbuf(f"picked{r}_{first}", [P, count * P], F32)
             nc.vector.tensor_copy(picked[:], y_sb[:].indirect(entries(pos_sb[r], first * P, count * P)))
-            by_token = ring_bank(f"by_token{r}_{first}", [P, count, N])
+            by_token = own_bank(f"by_token{r}_{first}", [P, count, N], f"first{(CHOICES * (first // HALF_BLOCKS) + r) % 3}")
             scaled = sbuf(f"scaled{r}_{first}", [P, count, N], F32)
             for c in range(count):
                 nc.tensor.transpose(by_token[:, c, :], picked[:, c * P : (c + 1) * P], ident[:])
@@ -254,18 +251,25 @@ def tile_moe_mlr_silu_kernel(
                                      scale=gate_cols[:, column : column + 1])
             return [scaled[:, c, :] for c in range(count)]
 
-        halves = [[gated_choice(r, first, HALF_BLOCKS) for r in range(CHOICES)] for first in (0, HALF_BLOCKS)]
-        gated = [halves[0][r] + halves[1][r] for r in range(CHOICES)]
-        scatter(adapted, FIRST_SCATTER, F * D - FIRST_SCATTER)
+        o_ps = [own_bank(f"o_ps{half}", [P, HALF_BLOCKS * P], tag) for half, tag in enumerate(("c", "d"))]
 
-        for half, tag in enumerate(("c", "d")):
-            o_ps = own_bank(f"o_ps{half}", [P, HALF_BLOCKS * P], tag)
-            for r in range(CHOICES):
-                for c in range(HALF_BLOCKS):
-                    nc.tensor.matmul(o_ps[:, c * P : (c + 1) * P], gated[r][HALF_BLOCKS * half + c], ident[:],
-                                     is_transpose=True, start=(r == 0 and c == 0),
-                                     stop=(r == CHOICES - 1 and c == HALF_BLOCKS - 1))
+        def turn_back(r, half, gated):
+            for c in range(HALF_BLOCKS):
+                nc.tensor.matmul(o_ps[half][:, c * P : (c + 1) * P], gated[c], ident[:], is_transpose=True,
+                                 start=(r == 0 and c == 0), stop=(r == CHOICES - 1 and c == HALF_BLOCKS - 1))
+
+        steps = [(r, half) for half in range(2) for r in range(CHOICES)]
+        gated = []
+        for step, (r, half) in enumerate(steps):
+            if step >= CHOICES:
+                turn_back(*steps[step - CHOICES], gated[step - CHOICES])
+            gated.append(gated_choice(r, half * HALF_BLOCKS, HALF_BLOCKS))
+        scatter(adapted, FIRST_SCATTER, F * D - FIRST_SCATTER)
+        for step in range(len(steps) - CHOICES, len(steps)):
+            turn_back(*steps[step], gated[step])
+
+        for half in range(2):
             tokens = slice(half * HALF_BLOCKS * P, (half + 1) * HALF_BLOCKS * P)
             result = sbuf(f"result{half}", [P, HALF_BLOCKS * P], F32)
-            nc.vector.tensor_tensor(result[:], o_ps[:], adapted[:, tokens], ALU.add)
+            nc.vector.tensor_tensor(result[:], o_ps[half][:], adapted[:, tokens], ALU.add)
             nc.sync.dma_start(out=out[:, tokens], in_=result[:])

@@ -240,7 +240,11 @@ def tile_moe_mlr_silu_kernel(
 
         def gated_choice(r, first, count):
             picked = sbuf(f"picked{r}_{first}", [P, count * P], F32)
-            nc.vector.tensor_copy(picked[:], y_sb[:].indirect(entries(pos_sb[r], first * P, count * P)))
+            window = y_sb[:].indirect(entries(pos_sb[r], first * P, count * P))
+            if (r, first) == (1, 0):
+                nc.scalar.activation(out=picked[:], in_=window, func=ACT.Copy)
+            else:
+                nc.vector.tensor_copy(picked[:], window)
             by_token = own_bank(f"by_token{r}_{first}", [P, count, N], f"first{(CHOICES * (first // HALF_BLOCKS) + r) % 3}")
             scaled = sbuf(f"scaled{r}_{first}", [P, count, N], F32)
             for c in range(count):

@@ -25,7 +25,7 @@ SCALE_ROWS = 4
 MOVED_ROWS = 112
 WINDOW = 688
 PLANE_WINDOW = 1024 + 192
-FIRST_SCATTER = 256
+FIRST_SCATTER = 128
 SCATTER_WINDOW = 2 * (F * D - FIRST_SCATTER)
 PAIR = 2
 PAIR_SLOTS = PAIR * D
@@ -33,7 +33,7 @@ TOKEN_BLOCKS = T // P
 HALF_BLOCKS = TOKEN_BLOCKS // 2
 
 EARLY = 4
-MIDDLE = 3
+MIDDLE = 2
 LAST = E - EARLY - MIDDLE
 LATE_PLANE = 1
 WORD_BYTES = 4
@@ -147,7 +147,7 @@ def tile_moe_mlr_silu_kernel(
                         rhs=wa_sb[pair][:, g * PASSES + s, :].bitcast(FP4X4), rhs_scale=wa_plane[:, f * PASSES + s, :],
                         start=(s == 0), stop=(s == PASSES - 1))
 
-        h_bf = [sbuf(f"h_bf{pair}", [P, 4 * PAIR_SLOTS], BF16) for pair in range(F // PAIR)]
+        h_bf = sbuf("h_bf", [P, 4 * F * D], BF16)
         y_sb = sbuf("y_sb", [P, E * C], F32, at=AT_Y)
         h_rows = [sbuf(f"h_rows{f}", [P, H], BF16) for f in range(F)]
 
@@ -161,9 +161,8 @@ def tile_moe_mlr_silu_kernel(
             for u in range(2):
                 nc.tensor.transpose(turned[:, u * D : (u + 1) * D],
                                     h_rows[f][:].bitcast(F32)[:, u * P : (u + 1) * P], ident[:])
-            pair, g = divmod(f, PAIR)
             nc.scalar.copy(
-                out=h_bf[pair][:].bitcast(F32).rearrange("p (g m u) -> p g m u", g=PAIR, u=2)[:, g],
+                out=h_bf[:].bitcast(F32).rearrange("p (f m u) -> p f m u", f=F, u=2)[:, f],
                 in_=turned[:].rearrange("p (u m) -> p m u", u=2))
 
         activate(0)
@@ -174,7 +173,7 @@ def tile_moe_mlr_silu_kernel(
         activate(3)
         turn(2, "c")
 
-        gate_turned = own_bank("gate_turned", [P, P], "b")
+        gate_turned = own_bank("gate_turned", [P, P], "a")
         nc.tensor.transpose(gate_turned[:], gate_rows[:], ident[:])
         gate_cols = sbuf("gate_cols", [P, CHOICES * TOKEN_BLOCKS], F32)
         nc.scalar.copy(out=gate_cols[:], in_=gate_turned[:, 0 : CHOICES * TOKEN_BLOCKS])
@@ -188,33 +187,33 @@ def tile_moe_mlr_silu_kernel(
 
         def experts(first, count, words, planes, tag):
             y_ps = own_bank(f"y_ps{first}", [P, count * C], tag)
-            for g in range(count):
-                half, place = divmod(first + g, E // 2)
-                slots = slice(g * C, (g + 1) * C)
-                for s in range(PASSES):
+            for s in range(PASSES):
+                for g in range(count):
+                    half, place = divmod(first + g, E // 2)
+                    slots = slice(g * C, (g + 1) * C)
                     nc.tensor.matmul_mx(
                         out=y_ps[:, slots],
                         lhsT=w_sb[half][:, place * PASSES + s, :].bitcast(FP8X4),
                         lhsT_scale=w_plane[:, (first + g) * PASSES + s, :],
                         rhs=words[s][:, slots].bitcast(FP8X4),
                         rhs_scale=planes[first + g][SCALE_ROWS * s : P, :],
-                        start=(s == 0), stop=(s == PASSES - 1))
+                        start=(s == 0 and g == 0), stop=(s == PASSES - 1 and g == count - 1))
             return lambda: nc.scalar.copy(out=y_sb[:, first * C : (first + count) * C], in_=y_ps[:])
 
         z_sb = sbuf("z_sb", [P, F * D], F32)
 
-        def second_layer(pair, tag):
-            h_codes = sbuf(f"h_codes{pair}", [P, PAIR_SLOTS], U32, at=AT_Y if pair == 0 else None)
-            h_plane = sbuf(f"h_plane{pair}", [P, PAIR_SLOTS], U8)
-            z_ps = own_bank(f"z_ps{pair}", [P, PAIR_SLOTS], tag)
-            nc.vector.quantize_mx(out=h_codes[:].bitcast(FP8X4), scales=h_plane[:], in_=h_bf[pair][:])
-            for g in range(PAIR):
-                f = PAIR * pair + g
+        def second_layer(first, count, tag):
+            h_codes = sbuf(f"h_codes{first}", [P, count * D], U32, at=AT_Y if first == 0 else None)
+            h_plane = sbuf(f"h_plane{first}", [P, count * D], U8)
+            z_ps = own_bank(f"z_ps{first}", [P, count * D], tag)
+            nc.vector.quantize_mx(out=h_codes[:].bitcast(FP8X4), scales=h_plane[:],
+                                  in_=h_bf[:, 4 * first * D : 4 * (first + count) * D])
+            for g in range(count):
                 slots = slice(g * D, (g + 1) * D)
                 nc.tensor.matmul_mx(
-                    out=z_ps[:, slots], lhsT=wb_sb[:, f, :].bitcast(FP4X4), lhsT_scale=wb_plane[:, f, :],
+                    out=z_ps[:, slots], lhsT=wb_sb[:, first + g, :].bitcast(FP4X4), lhsT_scale=wb_plane[:, first + g, :],
                     rhs=h_codes[:, slots].bitcast(FP8X4), rhs_scale=h_plane[:, slots], start=True, stop=True)
-            nc.scalar.copy(out=z_sb[:, pair * PAIR_SLOTS : (pair + 1) * PAIR_SLOTS], in_=z_ps[:])
+            nc.scalar.copy(out=z_sb[:, first * D : (first + count) * D], in_=z_ps[:])
 
         def scatter(adapted, first, count):
             nc.vector.tensor_tensor(adapted[:].indirect(entries(offs2_sb, first, count)),
@@ -225,7 +224,7 @@ def tile_moe_mlr_silu_kernel(
         early_words = [gather_slots(f"early_words{s}", x_windows[s], 0, EARLY, U32) for s in range(PASSES)]
         early_copy = experts(0, EARLY, early_words, planes, "b")
         late_words0 = gather_slots("late_words0", x_windows[0], EARLY, E - EARLY, U32)
-        second_layer(0, "d")
+        second_layer(0, 1, "d")
         early_copy()
         last_plane = gather_slots("last_plane", x_plane[:, 0:T], E - LATE_PLANE, LATE_PLANE, U8, at=AT_LAST_PLANE)
         planes.extend(last_plane[:, e * C : (e + 1) * C] for e in range(LATE_PLANE))
@@ -236,41 +235,41 @@ def tile_moe_mlr_silu_kernel(
 
         adapted = sbuf("adapted", [P, SCATTER_WINDOW], F32, at=AT_X_PLANE)
         scatter(adapted, 0, FIRST_SCATTER)
-        second_layer(1, "a")
-
-        def gated_choice(r, first, count):
-            picked = sbuf(f"picked{r}_{first}", [P, count * P], F32)
-            window = y_sb[:].indirect(entries(pos_sb[r], first * P, count * P))
-            if (r, first) == (1, 0):
-                nc.scalar.activation(out=picked[:], in_=window, func=ACT.Copy)
-            else:
-                nc.vector.tensor_copy(picked[:], window)
-            by_token = own_bank(f"by_token{r}_{first}", [P, count, N], f"first{(CHOICES * (first // HALF_BLOCKS) + r) % 3}")
-            scaled = sbuf(f"scaled{r}_{first}", [P, count, N], F32)
-            for c in range(count):
-                nc.tensor.transpose(by_token[:, c, :], picked[:, c * P : (c + 1) * P], ident[:])
-            for c in range(count):
-                column = r * TOKEN_BLOCKS + first + c
-                nc.scalar.activation(out=scaled[:, c, :], in_=by_token[:, c, :], func=ACT.Copy,
-                                     scale=gate_cols[:, column : column + 1])
-            return [scaled[:, c, :] for c in range(count)]
+        second_layer(1, F - 1, "c")
 
         o_ps = [own_bank(f"o_ps{half}", [P, HALF_BLOCKS * P], tag) for half, tag in enumerate(("c", "d"))]
 
-        def turn_back(r, half, gated):
+        def choice(r, half):
+            picked = sbuf(f"picked{r}_{half}", [P, HALF_BLOCKS * P], F32)
+            window = y_sb[:].indirect(entries(pos_sb[r], half * HALF_BLOCKS * P, HALF_BLOCKS * P))
+            if r == 0:
+                nc.vector.tensor_copy(picked[:], window)
+            else:
+                nc.scalar.activation(out=picked[:], in_=window, func=ACT.Copy)
+            by_token = own_bank(f"by_token{r}_{half}", [P, HALF_BLOCKS, N], f"first{CHOICES * half + r}")
             for c in range(HALF_BLOCKS):
-                nc.tensor.matmul(o_ps[half][:, c * P : (c + 1) * P], gated[c], ident[:], is_transpose=True,
+                nc.tensor.transpose(by_token[:, c, :], picked[:, c * P : (c + 1) * P], ident[:])
+            return by_token
+
+        def gate_and_turn_back(r, half, by_token):
+            scaled = sbuf(f"scaled{r}_{half}", [P, HALF_BLOCKS, N], F32)
+            column = r * TOKEN_BLOCKS + half * HALF_BLOCKS
+            if r == CHOICES:
+                nc.vector.tensor_tensor(
+                    scaled[:], by_token[:],
+                    gate_cols[:, column : column + HALF_BLOCKS].unsqueeze(2).to_broadcast([P, HALF_BLOCKS, N]), ALU.mult)
+            else:
+                for c in range(HALF_BLOCKS):
+                    nc.scalar.activation(out=scaled[:, c, :], in_=by_token[:, c, :], func=ACT.Copy,
+                                         scale=gate_cols[:, column + c : column + c + 1])
+            for c in range(HALF_BLOCKS):
+                nc.tensor.matmul(o_ps[half][:, c * P : (c + 1) * P], scaled[:, c, :], ident[:], is_transpose=True,
                                  start=(r == 0 and c == 0), stop=(r == CHOICES - 1 and c == HALF_BLOCKS - 1))
 
-        steps = [(r, half) for half in range(2) for r in range(CHOICES)]
-        gated = []
-        for step, (r, half) in enumerate(steps):
-            if step >= CHOICES:
-                turn_back(*steps[step - CHOICES], gated[step - CHOICES])
-            gated.append(gated_choice(r, half * HALF_BLOCKS, HALF_BLOCKS))
+        by_token = {(r, half): choice(r, half) for half in range(2) for r in range(CHOICES)}
         scatter(adapted, FIRST_SCATTER, F * D - FIRST_SCATTER)
-        for step in range(len(steps) - CHOICES, len(steps)):
-            turn_back(*steps[step], gated[step])
+        for r, half in by_token:
+            gate_and_turn_back(r, half, by_token[r, half])
 
         for half in range(2):
             tokens = slice(half * HALF_BLOCKS * P, (half + 1) * HALF_BLOCKS * P)

@@ -24,7 +24,7 @@ QUADRANT = 32
 SCALE_ROWS = 4
 MOVED_ROWS = 112
 WINDOW = 688
-PLANE_WINDOW = 1024 + 192
+PLANE_WINDOW = 1408
 FIRST_SCATTER = 128
 SCATTER_WINDOW = 2 * (F * D - FIRST_SCATTER)
 PAIR = 2
@@ -35,7 +35,7 @@ HALF_BLOCKS = TOKEN_BLOCKS // 2
 EARLY = 4
 MIDDLE = 2
 LAST = E - EARLY - MIDDLE
-LATE_PLANE = 1
+LATE_PLANE = 0
 WORD_BYTES = 4
 
 AT_MIDDLE_WORDS = 0
@@ -165,12 +165,10 @@ def tile_moe_mlr_silu_kernel(
                 out=h_bf[:].bitcast(F32).rearrange("p (f m u) -> p f m u", f=F, u=2)[:, f],
                 in_=turned[:].rearrange("p (u m) -> p m u", u=2))
 
-        activate(0)
-        activate(1)
+        for f in range(F):
+            activate(f)
         turn(0, "a")
         turn(1, "b")
-        activate(2)
-        activate(3)
         turn(2, "c")
 
         gate_turned = own_bank("gate_turned", [P, P], "a")
@@ -178,7 +176,7 @@ def tile_moe_mlr_silu_kernel(
         gate_cols = sbuf("gate_cols", [P, CHOICES * TOKEN_BLOCKS], F32)
         nc.scalar.copy(out=gate_cols[:], in_=gate_turned[:, 0 : CHOICES * TOKEN_BLOCKS])
 
-        turn(3, "a")
+        turn(3, "d")
 
         def gather_slots(name, window, first, count, dtype, at=None):
             gathered = sbuf(name, [P, count * C], dtype, at=at)
@@ -219,15 +217,13 @@ def tile_moe_mlr_silu_kernel(
             nc.vector.tensor_tensor(adapted[:].indirect(entries(offs2_sb, first, count)),
                                     z_sb[:, first : first + count], gate2_sb[:, first : first + count], ALU.mult)
 
-        plane = gather_slots("plane", x_plane[:], 0, E - LATE_PLANE, U8)
-        planes = [plane[:, e * C : (e + 1) * C] for e in range(E - LATE_PLANE)]
+        plane = gather_slots("plane", x_plane[:], 0, E, U8)
+        planes = [plane[:, e * C : (e + 1) * C] for e in range(E)]
         early_words = [gather_slots(f"early_words{s}", x_windows[s], 0, EARLY, U32) for s in range(PASSES)]
         early_copy = experts(0, EARLY, early_words, planes, "b")
         late_words0 = gather_slots("late_words0", x_windows[0], EARLY, E - EARLY, U32)
-        second_layer(0, 1, "d")
+        second_layer(0, 1, "first0")
         early_copy()
-        last_plane = gather_slots("last_plane", x_plane[:, 0:T], E - LATE_PLANE, LATE_PLANE, U8, at=AT_LAST_PLANE)
-        planes.extend(last_plane[:, e * C : (e + 1) * C] for e in range(LATE_PLANE))
         middle_words1 = gather_slots("middle_words1", x_windows[1], EARLY, MIDDLE, U32, at=AT_MIDDLE_WORDS)
         experts(EARLY, MIDDLE, [late_words0[:, 0 : MIDDLE * C], middle_words1], planes, "c")()
         last_words1 = gather_slots("last_words1", x_windows[1], EARLY + MIDDLE, LAST, U32, at=AT_LAST_WORDS)
@@ -237,7 +233,7 @@ def tile_moe_mlr_silu_kernel(
         scatter(adapted, 0, FIRST_SCATTER)
         second_layer(1, F - 1, "c")
 
-        o_ps = [own_bank(f"o_ps{half}", [P, HALF_BLOCKS * P], tag) for half, tag in enumerate(("c", "d"))]
+        o_ps = [own_bank(f"o_ps{half}", [P, HALF_BLOCKS * P], tag) for half, tag in enumerate(("b", "d"))]
 
         def choice(r, half):
             picked = sbuf(f"picked{r}_{half}", [P, HALF_BLOCKS * P], F32)

@@ -25,23 +25,21 @@ SCALE_ROWS = 4
 MOVED_ROWS = 112
 WINDOW = 688
 PLANE_WINDOW = 1408
-FIRST_SCATTER = 128
-SCATTER_WINDOW = 2 * (F * D - FIRST_SCATTER)
 PAIR = 2
-PAIR_SLOTS = PAIR * D
 TOKEN_BLOCKS = T // P
 HALF_BLOCKS = TOKEN_BLOCKS // 2
+WORD_BYTES = 4
+
+AHEAD = 1
+SCATTER_WINDOW = 2 * (F - AHEAD) * D
 
 EARLY = 4
 MIDDLE = 2
 LAST = E - EARLY - MIDDLE
-LATE_PLANE = 0
-WORD_BYTES = 4
 
 AT_MIDDLE_WORDS = 0
-AT_LAST_PLANE = AT_MIDDLE_WORDS + WORD_BYTES * MIDDLE * C
-AT_LAST_WORDS = AT_LAST_PLANE + LATE_PLANE * C
-AT_GATE_ROWS = AT_LAST_PLANE - (WORD_BYTES * P - LATE_PLANE * C) // 2
+AT_LAST_WORDS = AT_MIDDLE_WORDS + WORD_BYTES * MIDDLE * C
+AT_GATE_ROWS = AT_LAST_WORDS - WORD_BYTES * P // 2
 AT_X_PLANE = 4096
 AT_Y = 8192
 
@@ -97,10 +95,10 @@ def tile_moe_mlr_silu_kernel(
         nc.vector.memset(wb_plane[:].rearrange("p a n -> p (a n)").bitcast(I32), 0)
         nc.vector.tensor_scalar(ident[:], column_less_row[:], 0.0, None, ALU.is_equal)
 
-        def load_plane(plane, scales, queue):
+        def load_plane(plane, scales):
             rows = scales.rearrange("m s (q j) c -> j q (m s) c", j=SCALE_ROWS)
             for j in range(SCALE_ROWS):
-                queue.dma_start(out=plane[j:P:QUADRANT].bitcast(I32), in_=rows[j].bitcast(I32))
+                nc.sync.dma_start(out=plane[j:P:QUADRANT].bitcast(I32), in_=rows[j].bitcast(I32))
 
         x_view = x_words.rearrange("s p t d -> s p (t d)").bitcast(I32)
         wa_view = wa_words.rearrange("f s p b -> p (f s) b").bitcast(I32)
@@ -113,15 +111,15 @@ def tile_moe_mlr_silu_kernel(
         for s in range(PASSES):
             nc.sync.dma_start(out=x_sb[:, x_first[s] : x_first[s] + T], in_=x_view[s])
         nc.sync.dma_start(out=wa_sb[0][:].bitcast(I32), in_=wa_view[:, 0 : PAIR * PASSES, :])
-        load_plane(wa_plane[:], wa_scales, nc.sync)
+        load_plane(wa_plane[:], wa_scales)
         nc.sync.dma_start(offs_sb[:], offs)
         nc.sync.dma_start(out=wa_sb[1][:].bitcast(I32), in_=wa_view[:, PAIR * PASSES : F * PASSES, :])
         nc.sync.dma_start(out=gate_rows[0 : CHOICES * TOKEN_BLOCKS, :],
                           in_=gate[:, 0, :].rearrange("r (c t) -> r c t", t=P))
+        load_plane(w_plane[:], w_scales)
         nc.sync.dma_start(out=w_sb[0][:], in_=w_view[:, 0 : E // 2 * PASSES, :])
-        load_plane(w_plane[:], w_scales, nc.sync)
         nc.sync.dma_start(out=wb_sb[:].bitcast(I32), in_=wb_words.rearrange("f s p b -> p (f s) b").bitcast(I32))
-        load_plane(wb_plane[:], wb_scales, nc.sync)
+        load_plane(wb_plane[:], wb_scales)
         nc.sync.dma_start(out=w_sb[1][:], in_=w_view[:, E // 2 * PASSES : E * PASSES, :])
         nc.sync.dma_start(out=gate2_sb[:], in_=gate2)
         for r, pos in enumerate((pos1, pos2)):
@@ -183,7 +181,7 @@ def tile_moe_mlr_silu_kernel(
             nc.vector.tensor_copy(gathered[:], window.indirect(entries(offs_sb, first * C, count * C)))
             return gathered[:]
 
-        def experts(first, count, words, planes, tag):
+        def experts(first, count, words, tag):
             y_ps = own_bank(f"y_ps{first}", [P, count * C], tag)
             for s in range(PASSES):
                 for g in range(count):
@@ -194,7 +192,7 @@ def tile_moe_mlr_silu_kernel(
                         lhsT=w_sb[half][:, place * PASSES + s, :].bitcast(FP8X4),
                         lhsT_scale=w_plane[:, (first + g) * PASSES + s, :],
                         rhs=words[s][:, slots].bitcast(FP8X4),
-                        rhs_scale=planes[first + g][SCALE_ROWS * s : P, :],
+                        rhs_scale=plane[SCALE_ROWS * s : P, (first + g) * C : (first + g + 1) * C],
                         start=(s == 0 and g == 0), stop=(s == PASSES - 1 and g == count - 1))
             return lambda: nc.scalar.copy(out=y_sb[:, first * C : (first + count) * C], in_=y_ps[:])
 
@@ -218,20 +216,19 @@ def tile_moe_mlr_silu_kernel(
                                     z_sb[:, first : first + count], gate2_sb[:, first : first + count], ALU.mult)
 
         plane = gather_slots("plane", x_plane[:], 0, E, U8)
-        planes = [plane[:, e * C : (e + 1) * C] for e in range(E)]
         early_words = [gather_slots(f"early_words{s}", x_windows[s], 0, EARLY, U32) for s in range(PASSES)]
-        early_copy = experts(0, EARLY, early_words, planes, "b")
+        early_copy = experts(0, EARLY, early_words, "b")
         late_words0 = gather_slots("late_words0", x_windows[0], EARLY, E - EARLY, U32)
-        second_layer(0, 1, "first0")
+        second_layer(0, AHEAD, "first0")
         early_copy()
         middle_words1 = gather_slots("middle_words1", x_windows[1], EARLY, MIDDLE, U32, at=AT_MIDDLE_WORDS)
-        experts(EARLY, MIDDLE, [late_words0[:, 0 : MIDDLE * C], middle_words1], planes, "c")()
+        experts(EARLY, MIDDLE, [late_words0[:, 0 : MIDDLE * C], middle_words1], "c")()
         last_words1 = gather_slots("last_words1", x_windows[1], EARLY + MIDDLE, LAST, U32, at=AT_LAST_WORDS)
-        experts(EARLY + MIDDLE, LAST, [late_words0[:, MIDDLE * C : (E - EARLY) * C], last_words1], planes, "a")()
+        experts(EARLY + MIDDLE, LAST, [late_words0[:, MIDDLE * C : (E - EARLY) * C], last_words1], "a")()
 
         adapted = sbuf("adapted", [P, SCATTER_WINDOW], F32, at=AT_X_PLANE)
-        scatter(adapted, 0, FIRST_SCATTER)
-        second_layer(1, F - 1, "c")
+        scatter(adapted, 0, AHEAD * D)
+        second_layer(AHEAD, F - AHEAD, "c")
 
         o_ps = [own_bank(f"o_ps{half}", [P, HALF_BLOCKS * P], tag) for half, tag in enumerate(("b", "d"))]
 
@@ -242,28 +239,23 @@ def tile_moe_mlr_silu_kernel(
                 nc.vector.tensor_copy(picked[:], window)
             else:
                 nc.scalar.activation(out=picked[:], in_=window, func=ACT.Copy)
-            by_token = own_bank(f"by_token{r}_{half}", [P, HALF_BLOCKS, N], f"first{CHOICES * half + r}")
+            turned = own_bank(f"by_token{r}_{half}", [P, HALF_BLOCKS, N], f"first{CHOICES * half + r}")
             for c in range(HALF_BLOCKS):
-                nc.tensor.transpose(by_token[:, c, :], picked[:, c * P : (c + 1) * P], ident[:])
-            return by_token
+                nc.tensor.transpose(turned[:, c, :], picked[:, c * P : (c + 1) * P], ident[:])
+            return turned
 
-        def gate_and_turn_back(r, half, by_token):
+        def gate_and_turn_back(r, half, turned):
             scaled = sbuf(f"scaled{r}_{half}", [P, HALF_BLOCKS, N], F32)
             column = r * TOKEN_BLOCKS + half * HALF_BLOCKS
-            if r == CHOICES:
-                nc.vector.tensor_tensor(
-                    scaled[:], by_token[:],
-                    gate_cols[:, column : column + HALF_BLOCKS].unsqueeze(2).to_broadcast([P, HALF_BLOCKS, N]), ALU.mult)
-            else:
-                for c in range(HALF_BLOCKS):
-                    nc.scalar.activation(out=scaled[:, c, :], in_=by_token[:, c, :], func=ACT.Copy,
-                                         scale=gate_cols[:, column + c : column + c + 1])
+            for c in range(HALF_BLOCKS):
+                nc.scalar.activation(out=scaled[:, c, :], in_=turned[:, c, :], func=ACT.Copy,
+                                     scale=gate_cols[:, column + c : column + c + 1])
             for c in range(HALF_BLOCKS):
                 nc.tensor.matmul(o_ps[half][:, c * P : (c + 1) * P], scaled[:, c, :], ident[:], is_transpose=True,
                                  start=(r == 0 and c == 0), stop=(r == CHOICES - 1 and c == HALF_BLOCKS - 1))
 
         by_token = {(r, half): choice(r, half) for half in range(2) for r in range(CHOICES)}
-        scatter(adapted, FIRST_SCATTER, F * D - FIRST_SCATTER)
+        scatter(adapted, AHEAD * D, (F - AHEAD) * D)
         for r, half in by_token:
             gate_and_turn_back(r, half, by_token[r, half])
 

@@ -29,6 +29,7 @@ PAIR = 2
 TOKEN_BLOCKS = T // P
 HALF_BLOCKS = TOKEN_BLOCKS // 2
 WORD_BYTES = 4
+ON_VECTOR = 416
 
 AHEAD = 1
 SCATTER_WINDOW = 2 * (F - AHEAD) * D
@@ -234,11 +235,14 @@ def tile_moe_mlr_silu_kernel(
 
         def choice(r, half):
             picked = sbuf(f"picked{r}_{half}", [P, HALF_BLOCKS * P], F32)
-            window = y_sb[:].indirect(entries(pos_sb[r], half * HALF_BLOCKS * P, HALF_BLOCKS * P))
-            if r == 0:
-                nc.vector.tensor_copy(picked[:], window)
-            else:
-                nc.scalar.activation(out=picked[:], in_=window, func=ACT.Copy)
+            first = half * HALF_BLOCKS * P
+            on_vector = min(max(ON_VECTOR - first, 0), HALF_BLOCKS * P) if r == 0 else 0
+            if on_vector > 0:
+                nc.vector.tensor_copy(picked[:, 0:on_vector], y_sb[:].indirect(entries(pos_sb[r], first, on_vector)))
+            if on_vector < HALF_BLOCKS * P:
+                nc.scalar.activation(
+                    out=picked[:, on_vector : HALF_BLOCKS * P], func=ACT.Copy,
+                    in_=y_sb[:].indirect(entries(pos_sb[r], first + on_vector, HALF_BLOCKS * P - on_vector)))
             turned = own_bank(f"by_token{r}_{half}", [P, HALF_BLOCKS, N], f"first{CHOICES * half + r}")
             for c in range(HALF_BLOCKS):
                 nc.tensor.transpose(turned[:, c, :], picked[:, c * P : (c + 1) * P], ident[:])

from contextlib import ExitStack

import concourse.mybir as mybir

K, T, E, C, F, D, H, N = 1024, 512, 8, 128, 4, 128, 512, 128
FLOPS = 2 * K * N * E * C + 2 * K * H * F * D + 2 * H * N * F * D

F32 = mybir.dt.float32
BF16 = mybir.dt.bfloat16
I32 = mybir.dt.int32
U32 = mybir.dt.uint32
U16 = mybir.dt.uint16
U8 = mybir.dt.uint8
FP8X4 = mybir.dt.float8_e4m3fn_x4
FP4X4 = mybir.dt.float4_e2m1fn_x4
ACT = mybir.ActivationFunctionType
ALU = mybir.AluOpType

P = 128
PASSES = K // 512
CHOICES = 2
LIST_ROWS = 16
QUADRANT = 32
SCALE_ROWS = 4
MOVED_ROWS = 112
WINDOW = 688
PLANE_WINDOW = 1408
PAIR = 2
TOKEN_BLOCKS = T // P
HALF_BLOCKS = TOKEN_BLOCKS // 2
WORD_BYTES = 4
ON_VECTOR = 416

AHEAD = 1
SCATTER_WINDOW = 2 * (F - AHEAD) * D

EARLY = 4
MIDDLE = 2
LAST = E - EARLY - MIDDLE

AT_MIDDLE_WORDS = 0
AT_LAST_WORDS = AT_MIDDLE_WORDS + WORD_BYTES * MIDDLE * C
AT_GATE_ROWS = AT_LAST_WORDS - WORD_BYTES * P // 2
AT_X_PLANE = 4096
AT_Y = 8192


def tile_moe_mlr_silu_kernel(
    tc, x_words, x_scales, w_words, w_scales, wa_words, wa_scales, wb_words, wb_scales,
    gate, gate2, offs, pos1, pos2, offs2, out
):
    nc = tc.nc
    with ExitStack() as ctx:
        keep = ctx.enter_context(tc.tile_pool(name="keep", bufs=1))
        psum = ctx.enter_context(tc.psum_pool(name="psum", bufs=1))
        shared = ctx.enter_context(tc.tile_pool(name="shared", bufs=1))

        def sbuf(name, shape, dtype, at=None):
            if at is None:
                return keep.tile(shape, dtype, name=name, align_bytes=64)
            return shared.tile(shape, dtype, name=name, offset=at, align_bytes=64)

        def own_bank(name, shape, tag):
            return psum.tile(shape, F32, name=name, tag=tag)

        def entries(list_sb, first, count):
            return list_sb[:, first // LIST_ROWS : (first + count) // LIST_ROWS]

        offs_sb = keep.tile([P, E * C // LIST_ROWS], U16, name="offs_sb")
        offs2_sb = keep.tile([P, F * D // LIST_ROWS], U16, name="offs2_sb")
        pos_sb = [keep.tile([P, T // LIST_ROWS], U16, name=f"pos_sb{r}") for r in range(CHOICES)]

        x_sb = sbuf("x_sb", [P, T + WINDOW], I32)
        x_first = [(PASSES - 1 - s) * T for s in range(PASSES)]
        x_plane = sbuf("x_plane", [P, PLANE_WINDOW], U8, at=AT_X_PLANE)
        wa_sb = [sbuf(f"wa_sb{pair}", [P, PAIR * PASSES, 2 * H], U8) for pair in range(F // PAIR)]
        wa_plane = sbuf("wa_plane", [P, F * PASSES, H], U8)
        w_sb = [sbuf(f"w_sb{half}", [P, E // 2 * PASSES, N], I32) for half in range(2)]
        w_plane = sbuf("w_plane", [P, E * PASSES, N], U8)
        wb_sb = sbuf("wb_sb", [P, F, 2 * N], U8)
        wb_plane = sbuf("wb_plane", [P, F, N], U8)
        gate_rows = sbuf("gate_rows", [P, P], F32, at=AT_GATE_ROWS)
        gate2_sb = sbuf("gate2_sb", [P, F * D], F32)
        ident = sbuf("ident", [P, P], F32)
        a_planes = [sbuf(f"a_plane{s}", [P, F * D], U8) for s in range(PASSES)]

        column_less_row = sbuf("column_less_row", [P, P], I32)
        nc.gpsimd.iota(column_less_row[:], [[1, P]], base=0, channel_multiplier=-1)
        nc.vector.memset(x_plane[:, 0 : T + WORD_BYTES].bitcast(I32), 0)
        nc.vector.memset(wa_plane[:].rearrange("p a i -> p (a i)").bitcast(I32), 0)
        nc.vector.memset(x_plane[:, T + WORD_BYTES : PLANE_WINDOW].bitcast(I32), 0)
        nc.vector.memset(x_sb[:, PASSES * T : T + WINDOW], 0)
        nc.vector.memset(a_planes[1][:].bitcast(I32), 0)
        nc.vector.memset(gate_rows[:], 0.0)
        nc.vector.memset(w_plane[:].rearrange("p a n -> p (a n)").bitcast(I32), 0)
        nc.vector.memset(wb_plane[:].rearrange("p a n -> p (a n)").bitcast(I32), 0)
        nc.vector.tensor_scalar(ident[:], column_less_row[:], 0.0, None, ALU.is_equal)

        def load_plane(plane, scales):
            rows = scales.rearrange("m s (q j) c -> j q (m s) c", j=SCALE_ROWS)
            for j in range(SCALE_ROWS):
                nc.sync.dma_start(out=plane[j:P:QUADRANT].bitcast(I32), in_=rows[j].bitcast(I32))

        x_view = x_words.rearrange("s p t d -> s p (t d)").bitcast(I32)
        wa_view = wa_words.rearrange("f s p b -> p (f s) b").bitcast(I32)
        w_view = w_words.rearrange("e s p n d -> p (e s) (n d)").bitcast(I32)
        nc.sync.dma_start(offs2_sb[:], offs2)
        for q in range(P // QUADRANT):
            (nc.sync, nc.scalar)[q % 2].dma_start(
                out=x_plane[QUADRANT * q : QUADRANT * q + PASSES * SCALE_ROWS, 0:T].bitcast(I32),
                in_=x_scales[:, SCALE_ROWS * q : SCALE_ROWS * (q + 1), :].bitcast(I32))
        for s in range(PASSES):
            nc.sync.dma_start(out=x_sb[:, x_first[s] : x_first[s] + T], in_=x_view[s])
        nc.sync.dma_start(out=wa_sb[0][:].bitcast(I32), in_=wa_view[:, 0 : PAIR * PASSES, :])
        load_plane(wa_plane[:], wa_scales)
        nc.sync.dma_start(offs_sb[:], offs)
        nc.sync.dma_start(out=wa_sb[1][:].bitcast(I32), in_=wa_view[:, PAIR * PASSES : F * PASSES, :])
        nc.sync.dma_start(out=gate_rows[0 : CHOICES * TOKEN_BLOCKS, :],
                          in_=gate[:, 0, :].rearrange("r (c t) -> r c t", t=P))
        load_plane(w_plane[:], w_scales)
        nc.sync.dma_start(out=w_sb[0][:], in_=w_view[:, 0 : E // 2 * PASSES, :])
        nc.sync.dma_start(out=wb_sb[:].bitcast(I32), in_=wb_words.rearrange("f s p b -> p (f s) b").bitcast(I32))
        load_plane(wb_plane[:], wb_scales)
        nc.sync.dma_start(out=w_sb[1][:], in_=w_view[:, E // 2 * PASSES : E * PASSES, :])
        nc.sync.dma_start(out=gate2_sb[:], in_=gate2)
        for r, pos in enumerate((pos1, pos2)):
            nc.sync.dma_start(pos_sb[r][:], pos)

        x_windows = [x_sb[:, x_first[s] : x_first[s] + WINDOW].bitcast(U32) for s in range(PASSES)]
        a_words = [sbuf(f"a_words{s}", [P, F * D], U32) for s in range(PASSES)]
        nc.vector.tensor_copy(a_planes[0][:], x_plane[:].indirect(offs2_sb[:]))
        nc.scalar.dma_start(out=a_planes[1][0:MOVED_ROWS, :].bitcast(I32),
                            in_=a_planes[0][SCALE_ROWS : SCALE_ROWS + MOVED_ROWS, :].bitcast(I32))
        for s in range(PASSES):
            nc.vector.tensor_copy(a_words[s][:], x_windows[s].indirect(offs2_sb[:]))

        pre = [own_bank(f"pre{f}", [P, H], f"first{f}") for f in range(F)]
        for pair in range(F // PAIR):
            for s in range(PASSES):
                for g in range(PAIR):
                    f = PAIR * pair + g
                    slots = slice(f * D, (f + 1) * D)
                    nc.tensor.matmul_mx(
                        out=pre[f][:],
                        lhsT=a_words[s][:, slots].bitcast(FP8X4), lhsT_scale=a_planes[s][:, slots],
                        rhs=wa_sb[pair][:, g * PASSES + s, :].bitcast(FP4X4), rhs_scale=wa_plane[:, f * PASSES + s, :],
                        start=(s == 0), stop=(s == PASSES - 1))

        h_bf = sbuf("h_bf", [P, 4 * F * D], BF16)
        y_sb = sbuf("y_sb", [P, E * C], F32, at=AT_Y)
        h_rows = [sbuf(f"h_rows{f}", [P, H], BF16) for f in range(F)]

        def activate(f):
            nc.scalar.activation(
                out=h_rows[f][:].rearrange("m (u p e) -> m u p e", u=2, e=2),
                in_=pre[f][:].rearrange("m (p u e) -> m u p e", u=2, e=2), func=ACT.Silu)

        def turn(f, tag):
            turned = own_bank(f"turned{f}", [P, 2 * D], tag)
            for u in range(2):
                nc.tensor.transpose(turned[:, u * D : (u + 1) * D],
                                    h_rows[f][:].bitcast(F32)[:, u * P : (u + 1) * P], ident[:])
            nc.scalar.copy(
                out=h_bf[:].bitcast(F32).rearrange("p (f m u) -> p f m u", f=F, u=2)[:, f],
                in_=turned[:].rearrange("p (u m) -> p m u", u=2))

        for f in range(F):
            activate(f)
        turn(0, "a")
        turn(1, "b")
        turn(2, "c")

        gate_turned = own_bank("gate_turned", [P, P], "a")
        nc.tensor.transpose(gate_turned[:], gate_rows[:], ident[:])
        gate_cols = sbuf("gate_cols", [P, CHOICES * TOKEN_BLOCKS], F32)
        nc.scalar.copy(out=gate_cols[:], in_=gate_turned[:, 0 : CHOICES * TOKEN_BLOCKS])

        turn(3, "d")

        def gather_slots(name, window, first, count, dtype, at=None):
            gathered = sbuf(name, [P, count * C], dtype, at=at)
            nc.vector.tensor_copy(gathered[:], window.indirect(entries(offs_sb, first * C, count * C)))
            return gathered[:]

        def experts(first, count, words, tag):
            y_ps = own_bank(f"y_ps{first}", [P, count * C], tag)
            for s in range(PASSES):
                for g in range(count):
                    half, place = divmod(first + g, E // 2)
                    slots = slice(g * C, (g + 1) * C)
                    nc.tensor.matmul_mx(
                        out=y_ps[:, slots],
                        lhsT=w_sb[half][:, place * PASSES + s, :].bitcast(FP8X4),
                        lhsT_scale=w_plane[:, (first + g) * PASSES + s, :],
                        rhs=words[s][:, slots].bitcast(FP8X4),
                        rhs_scale=plane[SCALE_ROWS * s : P, (first + g) * C : (first + g + 1) * C],
                        start=(s == 0 and g == 0), stop=(s == PASSES - 1 and g == count - 1))
            return lambda: nc.scalar.copy(out=y_sb[:, first * C : (first + count) * C], in_=y_ps[:])

        z_sb = sbuf("z_sb", [P, F * D], F32)

        def second_layer(first, count, tag):
            h_codes = sbuf(f"h_codes{first}", [P, count * D], U32, at=AT_Y if first == 0 else None)
            h_plane = sbuf(f"h_plane{first}", [P, count * D], U8)
            z_ps = own_bank(f"z_ps{first}", [P, count * D], tag)
            nc.vector.quantize_mx(out=h_codes[:].bitcast(FP8X4), scales=h_plane[:],
                                  in_=h_bf[:, 4 * first * D : 4 * (first + count) * D])
            for g in range(count):
                slots = slice(g * D, (g + 1) * D)
                nc.tensor.matmul_mx(
                    out=z_ps[:, slots], lhsT=wb_sb[:, first + g, :].bitcast(FP4X4), lhsT_scale=wb_plane[:, first + g, :],
                    rhs=h_codes[:, slots].bitcast(FP8X4), rhs_scale=h_plane[:, slots], start=True, stop=True)
            nc.scalar.copy(out=z_sb[:, first * D : (first + count) * D], in_=z_ps[:])

        def scatter(adapted, first, count):
            nc.vector.tensor_tensor(adapted[:].indirect(entries(offs2_sb, first, count)),
                                    z_sb[:, first : first + count], gate2_sb[:, first : first + count], ALU.mult)

        plane = gather_slots("plane", x_plane[:], 0, E, U8)
        early_words = [gather_slots(f"early_words{s}", x_windows[s], 0, EARLY, U32) for s in range(PASSES)]
        early_copy = experts(0, EARLY, early_words, "b")
        late_words0 = gather_slots("late_words0", x_windows[0], EARLY, E - EARLY, U32)
        second_layer(0, AHEAD, "first0")
        early_copy()
        middle_words1 = gather_slots("middle_words1", x_windows[1], EARLY, MIDDLE, U32, at=AT_MIDDLE_WORDS)
        experts(EARLY, MIDDLE, [late_words0[:, 0 : MIDDLE * C], middle_words1], "c")()
        last_words1 = gather_slots("last_words1", x_windows[1], EARLY + MIDDLE, LAST, U32, at=AT_LAST_WORDS)
        experts(EARLY + MIDDLE, LAST, [late_words0[:, MIDDLE * C : (E - EARLY) * C], last_words1], "a")()

        adapted = sbuf("adapted", [P, SCATTER_WINDOW], F32, at=AT_X_PLANE)
        scatter(adapted, 0, AHEAD * D)
        second_layer(AHEAD, F - AHEAD, "c")

        o_ps = [own_bank(f"o_ps{half}", [P, HALF_BLOCKS * P], tag) for half, tag in enumerate(("b", "d"))]

        def choice(r, half):
            picked = sbuf(f"picked{r}_{half}", [P, HALF_BLOCKS * P], F32)
            first = half * HALF_BLOCKS * P
            on_vector = min(max(ON_VECTOR - first, 0), HALF_BLOCKS * P) if r == 0 else 0
            if on_vector > 0:
                nc.vector.tensor_copy(picked[:, 0:on_vector], y_sb[:].indirect(entries(pos_sb[r], first, on_vector)))
            if on_vector < HALF_BLOCKS * P:
                nc.scalar.activation(
                    out=picked[:, on_vector : HALF_BLOCKS * P], func=ACT.Copy,
                    in_=y_sb[:].indirect(entries(pos_sb[r], first + on_vector, HALF_BLOCKS * P - on_vector)))
            turned = own_bank(f"by_token{r}_{half}", [P, HALF_BLOCKS, N], f"first{CHOICES * half + r}")
            for c in range(HALF_BLOCKS):
                nc.tensor.transpose(turned[:, c, :], picked[:, c * P : (c + 1) * P], ident[:])
            return turned

        def gate_and_turn_back(r, half, turned):
            scaled = sbuf(f"scaled{r}_{half}", [P, HALF_BLOCKS, N], F32)
            column = r * TOKEN_BLOCKS + half * HALF_BLOCKS
            for c in range(HALF_BLOCKS):
                nc.scalar.activation(out=scaled[:, c, :], in_=turned[:, c, :], func=ACT.Copy,
                                     scale=gate_cols[:, column + c : column + c + 1])
            for c in range(HALF_BLOCKS):
                nc.tensor.matmul(o_ps[half][:, c * P : (c + 1) * P], scaled[:, c, :], ident[:], is_transpose=True,
                                 start=(r == 0 and c == 0), stop=(r == CHOICES - 1 and c == HALF_BLOCKS - 1))

        by_token = {(r, half): choice(r, half) for half in range(2) for r in range(CHOICES)}
        scatter(adapted, AHEAD * D, (F - AHEAD) * D)
        for r, half in by_token:
            gate_and_turn_back(r, half, by_token[r, half])

        for half in range(2):
            tokens = slice(half * HALF_BLOCKS * P, (half + 1) * HALF_BLOCKS * P)
            result = sbuf(f"result{half}", [P, HALF_BLOCKS * P], F32)
            nc.vector.tensor_tensor(result[:], o_ps[half][:], adapted[:, tokens], ALU.add)
            nc.sync.dma_start(out=out[:, tokens], in_=result[:])
